import numpy as np, ml_dtypes
CORES = [242,247,114,119]
N = 4
BF = ml_dtypes.bfloat16
def gentries(a):
    return np.ascontiguousarray(a.reshape(8, 16, -1).transpose(0, 2, 1)).reshape(8, -1)
def gtable(e):
    e = np.asarray(e); return np.ascontiguousarray(e.reshape(8, -1, 16).transpose(0, 2, 1)).reshape(128, -1).astype(np.int32)
V, Q, T, S, HOP = 2048, 224, 3, 1, 1
TH, TAU = 1020, (1020, 1530, 1275)
def toward(rng, shape, hub, share):
    h = hub[np.arange(8).reshape((1, 8) + (1,) * (len(shape) - 2)), rng.integers(0, hub.shape[1], shape)]
    return np.where(rng.random(shape) < share, h, rng.integers(0, V, shape))
def parts(rng):
    hub = rng.integers(0, V, (8, 32))
    X = rng.integers(0, 256, (N, 8, 16, V)); E = toward(rng, (N, 8, 16, V), hub, 0.1)
    v = toward(rng, (N, 8, Q), hub, 0.2); z = rng.integers(0, 256, (N, 8, 16, Q)); L = toward(rng, (N, 8, 16, Q), hub, 0.3)
    return X, E, v, z, L
def pack(X, E, v, z, L):
    return {"X": np.ascontiguousarray(X.reshape(N, 128, V)).astype(np.float32).astype(BF), "E": np.ascontiguousarray(E.reshape(N, 128, V)).astype(np.int32),
            "v0": np.stack([gtable(a) for a in v]), "z0": np.ascontiguousarray(z.reshape(N, 128, Q)).astype(np.float32).astype(BF), "L0": np.ascontiguousarray(L.reshape(N, 128, Q)).astype(np.int32)}
def setup_inputs(rng):
    return pack(*parts(rng))
def skew(rng, shape):
    col = shape[:2] + (1, shape[3])
    x = np.minimum((np.exp2(8 * rng.random(col)) * rng.random(shape)).astype(np.int64), 255)
    return np.where(rng.random(shape) < 0.5 * rng.integers(0, 2, col), 255 - x, x)
def lean(rng, shape):
    u = rng.random(shape); i = np.minimum((V * u * u * u).astype(np.int64), V - 1)
    return np.where(rng.random(shape[:2] + (1,) * (len(shape) - 2)) < 0.5, V - 1 - i, i)
def setup_inputs_spread(rng):
    return pack(skew(rng, (N, 8, 16, V)), lean(rng, (N, 8, 16, V)), lean(rng, (N, 8, Q)), skew(rng, (N, 8, 16, Q)), lean(rng, (N, 8, 16, Q)))
def setup_inputs_ends(rng):
    X, E, v, z, L = parts(rng)
    X = 255 * (rng.random(X.shape) < rng.choice(np.array([0.1, 0.5, 0.9]), (N, 8, 1, V))).astype(np.int64)
    z = 255 * (rng.random(z.shape) < rng.choice(np.array([0.0, 0.25, 0.5, 0.75, 1.0]), (N, 8, 1, Q))).astype(np.int64)
    E, v, L = [np.where(rng.random(a.shape) < 0.75, (V - 1) * rng.integers(0, 2, a.shape), a) for a in (E, v, L)]
    X[..., [0, 1, V - 3]] = 0; X[..., [2, V - 2, V - 1]] = 255
    for g in range(8):
        tie, full = (V - 1, V - 2) if g % 2 == 0 else (V - 2, V - 1)
        E[:, g, :, tie] = np.array([2, V - 1, V - 2, V - 1] * 4); E[:, g, :, full] = V - 1
        E[:, g, :, 1] = np.array([V - 3, 0, 1, 0] * 4); E[:, g, :, V - 3] = 0; E[:, g, :, 2] = np.array([V - 1, 2] * 8)
        if g % 4 != 2: E[:, g, 0, 0] = V - 1; E[:, g, 1, 0] = 0
    v[..., Q - 1] = V - 1; v[..., Q - 2] = V - 2; z[..., Q - 2:] = 0; L[..., Q - 2:] = V - 1; L[:, :, 15, Q - 2:] = 0
    v[..., 0] = 1; z[..., 0] = 255; v[..., 1] = 1; z[..., 1] = 0
    return pack(X, E, v, z, L)
def setup_inputs_corners(rng):
    X, E, v, z, L = parts(rng); own = np.arange(V); kinds = rng.permutation(8); h = V // 2
    for g in range(8):
        e, l, k = E[:, g], L[:, g], int(kinds[g])
        if k == 0: e[:] = own
        elif k == 1: e[:, 0::2] = (own + 1) % V; e[:, 1::2] = (own - 1) % V
        elif k == 2: e[:] = 0; e[:, 0] = V - 1
        elif k == 3:
            w = int(rng.choice(np.array([0, V - 1, h]))); l[:] = w; z[:, g] = 0
            e[:, 1] = e[:, 0]
            e[:, 0::2, w] = 5; e[:, 1::2, w] = 6; X[:, g, :, 5] = 255; X[:, g, :, 6] = 0
        elif k == 4: v[:, g] = V - 1; l[:] = V - 1
        elif k == 5:
            few = rng.permutation(h)[:64]; x = X[:, g]; x[:] = rng.integers(70, 256, x.shape)
            x[:, :, few[:32]] = rng.integers(240, 256, (N, 16, 32)); x[:, :, few[32:]] = rng.integers(70, 81, (N, 16, 32))
            e[:] = rng.integers(0, h, e.shape); e[:, 1, :h] = e[:, 0, :h]; z[:, g] = 0
            e[:, 0, h:] = few[rng.integers(0, 32, (N, V - h))]; e[:, 1, h:] = few[rng.integers(32, 64, (N, V - h))]
            l[:, :15] = rng.integers(0, h, (N, 15, Q)); l[:, 15] = rng.integers(h, V, (N, Q))
        elif k == 6: z[:, g] = 255; z[int(rng.integers(0, N)), g] = 0
        else:
            c = V // 4; o = rng.permutation(V).reshape(4, c); x = X[:, g]; z[:, g] = 255
            for i in range(4): e[:, :, o[i]] = o[i][rng.integers(0, c, (N, 16, c))]
            x[:, :, o[0]] = rng.integers(0, 64, (N, 16, c))
            x[:, :, o[1]] = rng.integers(252, 256, (N, 16, c)); x[:, :5, o[1]] = rng.integers(0, 16, (N, 5, c))
            x[:, :, o[2]] = np.array([0] * 5 + [255] * 2 + [215] * 2 + [255] * 7)[:, None]
            x[:, :, o[3]] = np.array([0] * 4 + [254] + [255] * 11)[:, None]
    v[..., 0] = 0; v[..., Q - 1] = V - 1
    return pack(X, E, v, z, L)
def setup_inputs_crowd(rng):
    X, E, v, z, L = parts(rng); A = T * S
    kinds = np.stack([rng.permutation(np.array([0, 1, 2, 4])), rng.permutation(np.array([0, 1, 3, 4]))], axis=1).reshape(-1)
    for g in range(8):
        k = int(kinds[g])
        if k == 4: continue
        h = V // 2; four = np.array([0, V - 1, 1 + 2 * int(rng.integers(0, V // 4)), h + 2 * int(rng.integers(0, V // 4))])
        o = rng.permutation(np.setdiff1d(np.arange(V), four))
        hi = np.concatenate([four, o[:h - 4]]); lo = o[h - 4:]
        w = X[:, g]; w[:, :, hi] = rng.integers(240, 256, (N, 16, h)); w[:, :, lo] = rng.integers(70, 81, (N, 16, h))
        z[:, g] = rng.integers(0, 4, (N, 16, Q))
        e = E[:, g]; e[:, :2] = lo[rng.integers(0, h, (N, 2, V))]
        if k < 2:
            hs = hi[:4]; names = np.repeat(hs[(np.arange(N) + int(rng.integers(0, 4))) % 4][:, None], Q, axis=1)
            if k == 1:
                miss = rng.integers(0, Q, N); miss[int(rng.integers(0, N))] = Q - 1; names[np.arange(N), miss] = -1
        elif k == 2:
            hs = hi[:4]; names = rng.choice(hs, (N, Q))
        else:
            hs = hi[rng.permutation(h)[:Q]]; names = np.stack([rng.permutation(hs) for _ in range(N)])
        n = len(hs)
        a = e[:, 0::2]; a[:, :, hs] = hi[rng.integers(4 if k < 2 else 0, h, (N, 8, n))]
        b = e[:, 1::2]; b[:, :, hs] = lo[rng.integers(0, h, (N, 8, n))]
        l = lo[rng.integers(0, h, (N, 16, Q))]
        here = np.argsort(np.argsort(rng.random((N, 16 - A, Q)), axis=1), axis=1) < T
        l[:, A:] = np.where(here & (names >= 0)[:, None], names[:, None], l[:, A:])
        L[:, g] = l
    return pack(X, E, v, z, L)
def setup_inputs_ties(rng):
    X, E, v, z, L = parts(rng); h = V // 2; o = rng.permutation(V); tw = np.zeros(V, np.int64); tw[o[:h]] = o[h:]; tw[o[h:]] = o[:h]
    X = 51 * rng.integers(0, 6, X.shape); z = 51 * rng.integers(0, 6, z.shape); X[..., o[:h]] = X[..., o[h:]]
    E[:, :, 8:] = tw[E[:, :, :8]]; E = np.ascontiguousarray(E[:, :, rng.permutation(16)])
    X[..., V - 2] = 0; X[:, :, 12:, V - 2] = 255; X[..., V - 4] = 0
    E[..., V - 1] = V - 2; E[..., V - 2] = V - 2; E[..., V - 3] = V - 4; E[:, :, 0, V - 3] = V - 2
    v[..., Q - 2:] = V - 1; z[..., Q - 2:] = 0; z[:, :, 0, Q - 2] = 51; L[..., Q - 2:] = V - 3
    return pack(X, E, v, z, L)
def check_inputs(d):
    bad = []
    for k, lo, hi in (("X", 0, 255), ("E", 0, V - 1), ("v0", 0, V - 1), ("z0", 0, 255), ("L0", 0, V - 1)):
        a = np.asarray(d[k]).astype(np.float64)
        if not (np.min(a) >= lo and np.max(a) <= hi and np.all(a == np.floor(a))): bad.append("range of " + k)
    return bad
def pick(tab, ix):
    return np.take_along_axis(tab, ix[:, None, :], 2)
def reference(X, E, v0, z0, L0):
    x = X.astype(np.float32).astype(np.int64).reshape(N, 8, 16, V); e = E.astype(np.int64).reshape(N, 8, 16, V)
    v = np.stack([gentries(a) for a in v0]).astype(np.int64)
    z = z0.astype(np.float32).astype(np.int64).reshape(N, 8, 16, Q); L = L0.astype(np.int64).reshape(N, 8, 16, Q)
    wt = (2 * np.arange(16) + 1)[None, :, None]
    for t in range(T):
        mark = np.zeros((N, 8, V), bool)
        for r in range(N):
            p = (r + HOP * t) % N; s = (p + HOP) % N; zr = z[r].copy(); vr = v[r].copy(); ll = L[r].copy()
            for step in range(S):
                c = pick(e[p], vr)
                far = np.add.reduce(np.abs(pick(x[p], c.reshape(8, -1)).reshape(8, 16, 16, Q) - zr[:, :, None, :]), axis=1)
                k = np.argmin(far, axis=1)
                vr = np.take_along_axis(c, k[:, None, :], 1)[:, 0]; ll[:, S * t + step] = vr
            like = np.min(far, axis=1) <= TH; xv = pick(x[p], vr)
            flat = ll.reshape(8, -1); a = np.take_along_axis(e[s][:, 0], flat, 1); b = np.take_along_axis(e[s][:, 1], flat, 1)
            zz = np.tile(zr, (1, 1, 16))
            gap = np.add.reduce(np.abs(np.maximum(pick(x[s], a), zz) - np.maximum(pick(x[s], b), zz)), axis=1).reshape(8, 16, Q)
            fail = gap > TAU[t]; some = np.any(fail, axis=1); f = np.argmax(fail, axis=1)
            cut = ~like & some; none = ~like & ~some
            u = np.take_along_axis(ll, f[:, None, :], 1)[:, 0]; base = np.take_along_axis(a.reshape(8, 16, Q), f[:, None, :], 1)[:, 0]
            gi, qi = np.nonzero(cut)
            mark[s, gi, u[gi, qi]] = True; ll[gi, f[gi, qi], qi] = base[gi, qi]
            half = (zr + xv) >> 1; h = np.add.reduce(half * wt, axis=1) & (V - 1)
            L[r] = ll; v[r] = np.where(cut, base, np.where(none, h, vr))
            z[r] = np.where(like[:, None, :], np.abs(zr - xv), np.where(none[:, None, :], half, zr))
        e = np.where(mark[:, :, None, :], np.roll(e, -1, axis=2), e)
    ya = np.add.reduce(e * (np.arange(16) + 1)[None, None, :, None], axis=2)
    return {"yv": v.astype(np.float32), "yz": z.reshape(N, 128, Q).astype(np.float32), "yl": L.reshape(N, 128, Q).astype(np.float32), "ya": ya.astype(np.float32)}

@@ -1,0 +1,551 @@
+from concourse.bass import DstId, RemoteDMATransfer
+from concourse.mybir import AluOpType, ActivationFunctionType
+
+ALU = AluOpType
+ACT = ActivationFunctionType
+V, Q, NV, HQ = 2048, 224, 3, 112
+TH, TAU = 1020, (1020, 1530, 1275)
+MAGIC = 12582912.0
+BIG = 4194304.0
+
+CFG = {
+    "wmode": ["ha", "ha", "ha"],
+    "smode": ["1123", "1123", "1123"],
+    "bias": {}, "seed": 1, "rounds": 150, "rl3": False, "faa": True, "kca": False, "tia": True, "zg": [16, 16, 16], "cs": 28, "cw": 28, "xav": 3,
+    "pe": 0.55, "hop": 110.0, "same": 70.0, "gat": 1.6, "sca": 3.9, "link": 2600.0, "peek": 30.0,
+}
+DT = {"bf": "bfloat16", "hf": "float16", "f32": "float32", "i32": "int32", "u16": "uint16"}
+
+
+def plan(cfg):
+    ops, top, acc, psacc = [], {a: 0 for a in DT}, {a: [] for a in DT}, {}
+    nps = [0]; tag = ["i"]
+    w2 = {"bf": True, "hf": True, "f32": False, "i32": False, "u16": True, "ps": False}
+
+    def tile(a, n):
+        lo = (top[a] + 15) // 16 * 16
+        top[a] = lo + n
+        return (a, lo, lo + n, 1, 128, None)
+
+    def ps():
+        nps[0] += 1
+        return ("ps", 0, 512, 1, 128, nps[0] - 1)
+
+    def sl(r, a, b, step=1, p=None):
+        return (r[0], r[1] + a, r[1] + b, step, r[4] if p is None else p, r[5])
+
+    def wd(r):
+        if r[0] == "ind": return 16 * wd(r[2])
+        return (r[2] - r[1] + r[3] - 1) // r[3]
+
+    def ind(win, off):
+        return ("ind", win, off)
+
+    def isref(x):
+        return isinstance(x, tuple)
+
+    def add(eng, kind, args, rd, wr, cost, lat=0.0):
+        me = len(ops); deps = {}
+        rr, ww = [], []
+        for r in rd:
+            if r[0] == "ind": rr += [r[1], r[2]]
+            else: rr.append(r)
+        for r in wr:
+            if r[0] == "ind": ww.append(r[1]); rr.append(r[2])
+            else: ww.append(r)
+        dma = kind in ("dma", "send")
+        tiles = []
+        for isw, lst in ((False, rr), (True, ww)):
+            for r in lst:
+                if r[0] == "dram": continue
+                if r[0] == "ps":
+                    tiles.append(r[5])
+                    for o, ow, lo, hi in psacc.setdefault(r[5], []):
+                        if o == me: continue
+                        hard = ops[o]["eng"] != eng or (ow and not isw and lo < r[2] and r[1] < hi)
+                        deps[o] = deps.get(o, False) or hard
+                    psacc[r[5]].append((me, isw, r[1], r[2]))
+                    continue
+                keep = []
+                for e in acc[r[0]]:
+                    o, ow, lo, hi, st = e
+                    if o != me and (ow or isw) and lo < r[2] and r[1] < hi and not (st == r[3] > 1 and (lo - r[1]) % st):
+                        deps[o] = True
+                        if isw and r[3] == 1 and r[4] == 128 and r[1] <= lo and hi <= r[2]: continue
+                    keep.append(e)
+                acc[r[0]] = keep + [(me, isw, r[1], r[2], r[3])]
+        ops.append({"eng": eng, "kind": kind, "args": args, "deps": deps, "cost": cost, "lat": lat, "dma": dma,
+                    "tiles": sorted(set(tiles)), "tag": tag[0]})
+
+    def vcost(out, ins, per):
+        if out[0] == "ind": return 50 + cfg["sca"] * wd(out)
+        if ins[0][0] == "ind": return 50 + cfg["gat"] * wd(out)
+        return max(64.0, per * wd(ins[0])) + 10
+
+    def cp(out, i):
+        add("V", "cp", (out, i), [i], [out], vcost(out, [i], 0.5 if i[0] != "ind" and out[0] != "ind" and w2[i[0]] and w2[out[0]] else 1))
+
+    def tt(out, a, b, op):
+        add("V", "tt", (out, a, b, op), [a, b], [out], vcost(out, [a, b], 1 if "ps" in (a[0], b[0]) else 2))
+
+    def ts(out, a, s1, op0, s2=None, op1=None):
+        add("V", "ts", (out, a, s1, s2, op0, op1), [a] + [s for s in (s1, s2) if isref(s)], [out],
+            vcost(out, [a], 0.5 if a[0] != "ind" and w2[a[0]] and w2[out[0]] else 1))
+
+    def scan(out, d0, d1, op0, op1):
+        add("V", "scan", (out, d0, d1, op0, op1), [d0, d1], [out], vcost(out, [d0], 0.5 if w2[d0[0]] and w2[d1[0]] and w2[out[0]] else 1))
+
+    def mset(out, c):
+        add("V", "mset", (out, c), [], [out], max(64, wd(out)))
+
+    def act(out, i, f=None, bias=0.0, scale=1.0):
+        add("A", "act", (out, i, f or ACT.Identity, bias, scale), [i] + [s for s in (bias, scale) if isref(s)], [out],
+            65 + cfg["gat"] * wd(out) if i[0] == "ind" else max(64, wd(out)) + 30)
+
+    def mm(lst):
+        c = sum(max(min(64, wd(m[1])), wd(m[2])) * (1 if w2[m[2][0]] else 4) * cfg["pe"] + 4 for m in lst)
+        add("P", "mm", lst, [m[1] for m in lst] + [m[2] for m in lst], [m[0] for m in lst], c, 60.0)
+
+    def grp(out, pairs, start=True, stop=True):
+        return [(out, a, b, start and j == 0, stop and j == len(pairs) - 1) for j, (a, b) in enumerate(pairs)]
+
+    def relist(out, W, src, n, start=True, stop=True):
+        return grp(out, [(W[m], sl(src, m, n, 16)) for m in range(16)], start, stop)
+
+    def iota(out, pat, base=0, cm=0):
+        add("G", "iota", (out, pat, base, cm), [], [out], 130 + 2 * wd(out))
+
+    def asel(out, i, pat, op, fill, base, cm):
+        add("G", "asel", (out, i, pat, op, fill, base, cm), [i], [out], 170 + 2 * wd(out))
+
+    def spread(dst, src, on_g):
+        for k in range(16):
+            if k < on_g: asel(sl(dst, k, 16 * HQ, 16), src, [[0, HQ]], ALU.is_gt, 0.0, 1, 0)
+            else: cp(sl(dst, k, 16 * HQ, 16), src)
+
+    def dma(eng, out, i, lat):
+        add(eng, "dma", (out, i), [i], [out], 60, lat)
+
+    def send(pairs, by):
+        add("G", "send", pairs, [p[0] for p in pairs], [p[1] for p in pairs], 300, cfg["link"] + by)
+
+    def dram(name, idx):
+        return ("dram", name, idx)
+
+    A_ = slice(None)
+    E = tile("i32", V); X = tile("bf", V); v0 = tile("i32", 16); L0 = tile("i32", Q)
+    z = [tile("bf", Q) for _ in range(NV)]
+    dma("A", sl(v0, 0, 14), dram("v0", (A_, A_)), 2000)
+    for j in range(2):
+        dma("S", sl(E, 1024 * j, 1024 * j + 1024), dram("E", (A_, slice(1024 * j, 1024 * j + 1024))), 3600 + 1800 * j)
+    dma("A", z[0], dram("z0", (A_, A_)), 2300)
+    dma("A", L0, dram("L0", (A_, A_)), 2600)
+    dma("S", X, dram("X", (A_, A_)), 7000)
+
+    pi = tile("i32", 16); iota(sl(pi, 0, 1), [[0, 1]], 0, 1)
+    col = tile("f32", Q); iota(col, [[1, Q]])
+    colk = tile("f32", 128); iota(colk, [[0, 8], [1, 16]])
+    colg = tile("f32", 128); iota(colg, [[16, 8], [0, 16]])
+    oi = tile("i32", 16); iota(sl(oi, 0, 8), [[16, 8]], 15); iota(sl(oi, 8, 16), [[1, 8]])
+    ou = tile("u16", 16); cp(ou, oi)
+    olast, obc = sl(ou, 0, 8), sl(ou, 8, 15)
+    C = tile("f32", 32)
+    cc = [sl(C, j, j + 1) for j in range(32)]
+    ki = tile("i32", 16); ts(sl(ki, 0, 1), sl(pi, 0, 1), 15, ALU.bitwise_and)
+    pf, kf, gb = cc[0], cc[1], cc[2]
+    cp(pf, sl(pi, 0, 1)); cp(kf, sl(ki, 0, 1)); tt(gb, pf, kf, ALU.subtract)
+    KE = tile("f32", 16); ts(KE, sl(col, 0, 16), kf, ALU.is_equal)
+    KN = tile("f32", 16); ts(KN, sl(col, 0, 16), kf, ALU.not_equal)
+    ke = [sl(KE, j, j + 1) for j in range(16)]; kn = [sl(KN, j, j + 1) for j in range(16)]
+    c128 = sl(col, 0, 128); k112 = sl(colk, 0, HQ)
+
+    def times(src, s):
+        t = tile("bf", wd(src)); act(t, src, None, 0.0, s); return t
+
+    def cuts(t):
+        return [sl(t, 15 - m, 143 - m) for m in range(16)]
+
+    def summed(a, parts):
+        p = sl(ps(), 0, 128); mm(grp(p, [(Ib, x) for x in parts])); t = tile(a, 128); act(t, p); return t
+    p8, g15 = cc[20], cc[3]; ts(p8, pf, 8.0, ALU.add); ts(g15, gb, 15.0, ALU.add)
+    Iw = tile("bf", 144); ts(Iw, sl(col, 0, 144), p8, ALU.is_equal)
+    Ib = Ih = sl(Iw, 8, 136); J = sl(Iw, 12, 140)
+    nIb, I2, I2k, nI2k, nI4k = [times(Ib, s) for s in (-1.0, 2.0, 2048.0, -2048.0, -4096.0)]
+    nIh = nIb
+    Ww = tile("bf", 144); ts(Ww, sl(col, 0, 144), g15, ALU.is_equal)
+    Wb = Wh = cuts(Ww); nWb, W0, W1 = cuts(times(Ww, -1.0)), cuts(times(Ww, ke[0])), cuts(times(Ww, ke[1]))
+    wt, nwt, k1 = cc[4], cc[5], cc[6]
+    ts(wt, kf, 2.0, ALU.mult, 1.0, ALU.add); ts(nwt, kf, -2.0, ALU.mult, -1.0, ALU.add); ts(k1, kf, 1.0, ALU.add)
+    Bb = Bh = tile("bf", 128); ts(Bb, colg, gb, ALU.is_equal)
+    nBb, nDB, R0, Wt, nWt = [times(Bb, s) for s in (-1.0, -2048.0, ke[0], wt, nwt)]
+    G32 = times(sl(Bb, 0, 128, 16), 32.0)
+    G64, nG32 = (times(G32, 2.0), times(G32, -1.0)) if any("m" in s for s in cfg["wmode"]) else (None, None)
+    Kc = tile("bf", HQ); act(Kc, k112, None, kf, 0.0)
+    rbig = tile("f32", 128); ts(rbig, colk, 0.0, ALU.is_equal, BIG, ALU.mult)
+    rzero = tile("bf", HQ); act(rzero, k112, ACT.Sign)
+    Tri = tile("bf", 128); tmpa = tile("bf", 128)
+    asel(tmpa, nBb, [[1, 128]], ALU.is_gt, 0.0, 0, -1); asel(Tri, tmpa, [[1, 128]], ALU.not_equal, 1.0, 0, -1)
+    TriD = tile("hf", HQ); ts(TriD, k112, kf, ALU.is_ge, 0.5, ALU.mult)
+    Qrow = tile("bf", Q); act(Qrow, col)
+    TriQ = [tile("hf", HQ) for _ in range(2)]; Qlist = [sl(tile("bf", 16), 0, 14) for _ in range(2)]
+    m3 = [tile("hf", 384) for _ in range(2)]
+    for h in range(2):
+        tt(TriQ[h], sl(Qrow, HQ * h, HQ * h + HQ), TriD, ALU.add)
+        act(sl(Qlist[h], 0, 7), sl(col, 0, 7), None, 0.0, 0.0); act(sl(Qlist[h], 7, 14), sl(col, 7 * h, 7 * h + 7), None, kf, 16.0)
+        for j in range(2): ts(sl(m3[h], 128 * j + HQ, 128 * j + 128), sl(col, 0, 16), 0.0, ALU.mult)
+    mid = tile("hf", HQ); ts(mid, k112, 0.0, ALU.mult, 0.5 - V // 2, ALU.add)
+    m012, m16, spare, m03 = cc[7], cc[8], cc[10], cc[11]
+    ts(m012, kf, 2.5, ALU.is_lt); ts(m03, kf, 3.5, ALU.is_lt)
+    tt(cc[12], ke[4], ke[5], ALU.add); ts(m16, cc[12], 16.0, ALU.mult); ts(spare, kf, float(V + Q), ALU.add)
+    Mi = summed("bf", [times(Ib, m03), times(Wb[6], k1), Wb[7]])
+    tt(cc[17], m03, ke[0], ALU.subtract); ts(cc[18], ke[0], 16.0, ALU.mult, ke[6], ALU.add); tt(cc[19], cc[18], ke[7], ALU.subtract)
+    Tm = summed("f32", [times(sl(Iw, 9, 137), cc[17]), times(sl(Iw, 7, 135), ke[4]), times(Wb[6], cc[19]), times(Wb[7], ke[7])])
+    pk = tile("f32", 512); iota(pk, [[0, 512]])
+    pre = [sl(pk, 128 * h, 128 * h + 128) for h in range(2)]; kc = [sl(pk, 256 + 128 * h, 384 + 128 * h) for h in range(2)]
+
+    zs = [tile("bf", Q) for _ in range(NV)]; Ls = [tile("u16", Q) for _ in range(NV)]
+    Lo_ = [tile("u16", Q) for _ in range(NV)]
+    vl = [tile("u16", 16) for _ in range(NV)]
+    ts(Lo_[0], L0, kn[0], ALU.mult)
+    send([(z[0], zs[0]), (Lo_[0], Ls[0])], 900)
+    for h in range(2): cp(sl(vl[0], 8 * h, 8 * h + 7), sl(v0, 7 * h, 7 * h + 7))
+
+    tag[0] = "t"
+    TW = V + Q + 16
+    M = tile("f32", TW); H = tile("bf", TW); Lw = tile("bf", TW); Ef = tile("hf", V); Xa = tile("bf", V)
+    for j in range(4): cp(sl(Ef, 512 * j, 512 * j + 512), sl(E, 512 * j, 512 * j + 512))
+    ab = tile("u16", 256)
+    for j, Wj in enumerate((W0, W1)):
+        p = sl(ps(), 0, 128); mm(relist(p, Wj, Ef, V)); cp(sl(ab, 128 * j, 128 * j + 128), p)
+    for j in range(4):
+        c0, o0 = 512 * j, 32 * j
+        (cp if cfg.get("xav", 0) > j else act)(sl(Xa, c0, c0 + 512), ind(X, sl(ab, o0, o0 + 32)))
+        tt(sl(H, c0, c0 + 512), ind(X, sl(ab, 128 + o0, 160 + o0)), sl(Xa, c0, c0 + 512), ALU.max)
+        tt(sl(Lw, c0, c0 + 512), ind(X, sl(ab, 128 + o0, 160 + o0)), sl(Xa, c0, c0 + 512), ALU.min)
+    tag[0] = "n"
+    for j in range(4):
+        p = ps(); mm(grp(p, [(Mi, sl(Ef, 512 * j, 512 * j + 512))])); act(sl(M, 512 * j, 512 * j + 512), p)
+    NB = 16 * HQ
+    xg = [tile("bf", NB) for _ in range(2)]; xd = [tile("bf", NB) for _ in range(2)]
+    sg = [[tile("bf", NB) for _ in range(2)] for _ in range(2)]; sm = [[tile("bf", NB) for _ in range(2)] for _ in range(2)]
+    zr = [tile("bf", NB) for _ in range(2)]; zw = [tile("bf", NB) for _ in range(2)]
+    fin = [tile("f32", 240) for _ in range(2)]; finl = [tile("f32", 240) for _ in range(2)]
+
+    for t in range(NV):
+        last = t == NV - 1
+        vcl = tile("hf", Q); dl = tile("bf", Q); vnl = tile("u16", 16)
+        for h in range(2):
+            mode = cfg["wmode"][t][h]; tag[0] = "w%d%d" % (t, h)
+            zh = sl(z[t], HQ * h, HQ * h + HQ); vh = sl(vl[t], 8 * h, 8 * h + 7)
+            c = tile("u16", HQ); cp(c, ind(E, vh))
+            if mode == "z":
+                for k in range(16): cp(sl(zw[h], k, NB, 16), zh)
+            cq = cfg["cw"]
+            for j in range(HQ // cq):
+                c0, c1 = 16 * cq * j, 16 * cq * (j + 1)
+                o, src = sl(xg[h], c0, c1), ind(X, sl(c, cq * j, cq * (j + 1)))
+                if mode == "z":
+                    tt(o, src, sl(zw[h], c0, c1), ALU.subtract); act(sl(xd[h], c0, c1), o, ACT.Abs)
+                else: (cp if mode == "v" or (mode == "h" and j % 2) else act)(o, src)
+            ch = tile("hf", HQ); cp(ch, c)
+            key = sl(ps(), 0, 128, 1, HQ)
+            ko = [sl(key, k, 128, 16) for k in range(16)]
+            xk = [sl(xg[h], k, NB, 16) for k in range(16)]; dk = [sl(xd[h], HQ * k, HQ * k + HQ) for k in range(16)]
+            if mode == "m":
+                zp = sl(ps(), 0, HQ); mm(grp(zp, [(Ib, zh)]))
+            for j in range(4):
+                ks = range(4 * j, 4 * j + 4)
+                head = [(key, Kc, Ib, True, False)] if j == 0 else []
+                end = t == 0 and j == 3
+                if mode == "m":
+                    for k in ks: tt(dk[k], xk[k], zp, ALU.max)
+                    mm(head + [m for k in ks for m in ((ko[k], xk[k], nG32, False, False), (ko[k], dk[k], G64, False, end and k == 15))])
+                elif mode == "z":
+                    mm(head + [(ko[k], sl(xd[h], k, NB, 16), G32, False, end and k == 15) for k in ks])
+                else:
+                    p = ps()
+                    mm([m for k in ks for m in grp(sl(p, HQ * (k % 4), HQ * (k % 4) + HQ), [(Ib, xk[k]), (nIb, zh)])])
+                    act(sl(xd[h], 448 * j, 448 * j + 448), sl(p, 0, 448), ACT.Abs)
+                    mm(head + [(ko[k], dk[k], G32, False, end and k == 15) for k in ks])
+            tag[0] = "x%d%d" % (t, h)
+            if t > 0:
+                fl = tile("bf", HQ); ts(fl, ind(sl(M, 0, V), vh), m16, ALU.mult)
+                mm([(key, fl, J, False, True)])
+            kch = sl(kc[h], 0, 128, 1, HQ)
+            if cfg["kca"]:
+                act(kch, key); scan(sl(pre[h], 0, 128, 1, HQ), sl(rbig, 0, 128, 1, HQ), kch, ALU.add, ALU.min)
+            else:
+                scan(sl(pre[h], 0, 128, 1, HQ), sl(rbig, 0, 128, 1, HQ), key, ALU.add, ALU.min); cp(kch, key)
+            hot = tile("hf", 128); tt(hot, ind(pre[h], olast), kc[h], ALU.is_equal)
+            oh = sl(ps(), 0, HQ); mm(grp(oh, [(sl(hot, 0, 128, 1, HQ), sl(Ih, 0, HQ, 1, HQ))]))
+            vc = tile("hf", HQ); tt(vc, oh, ch, ALU.mult)
+            p = sl(ps(), 0, 7); mm(relist(p, Wh, vc, HQ))
+            vn = tile("u16", 8); cp(sl(vn, 0, 7), p)
+            send([(sl(vn, 0, 7), sl(vnl, 8 * h, 8 * h + 7))], 0)
+            d = tile("bf", HQ); tt(d, ind(X, sl(vn, 0, 7)), zh, ALU.subtract)
+            send([(vc, sl(vcl, HQ * h, HQ * h + HQ)), (d, sl(dl, HQ * h, HQ * h + HQ))], 500)
+        ue = tile("u16", 16); uf = [tile("f32", 8) for _ in range(2)]; ubc = tile("f32", Q); mu = tile("hf", Q)
+        nls = [tile("u16", 16) for _ in range(2)]
+        for h in range(2):
+            mode = cfg["smode"][t][2 * h:2 * h + 2]; q0 = HQ * h; tag[0] = "s%d%d" % (t, h)
+            zh = sl(zs[t], q0, q0 + HQ); Lh = sl(Ls[t], q0, q0 + HQ); vw = sl(vcl, q0, q0 + HQ); d = sl(dl, q0, q0 + HQ)
+            vnh = sl(vnl, 8 * h, 8 * h + 7); qr = sl(Qrow, q0, q0 + HQ)
+            G = sl(ps(), 0, HQ); first = [True]
+            if "1" in mode:
+                spread(zr[h], zh, cfg["zg"][t])
+            if "2" in mode:
+                zp = sl(ps(), 0, HQ); mm(grp(zp, [(Ib, zh)]))
+            if mode.count("3") == 1:
+                mm(grp(G, [(Bb, zh), (nWb[t], zh)] if mode[0] == "3" else [(nBb, zh), (Wb[t], zh)], True, False)); first[0] = False
+            for i, (tab, Ws) in enumerate(((H, Wb), (Lw, nWb))):
+                win = sl(tab, 0, V)
+                cq = cfg["cs"]
+                for j in range(HQ // cq):
+                    o, off = sl(sg[h][i], 16 * cq * j, 16 * cq * (j + 1)), sl(Lh, cq * j, cq * (j + 1))
+                    if mode[i] == "1": tt(o, ind(win, off), sl(zr[h], 16 * cq * j, 16 * cq * (j + 1)), ALU.max)
+                    else: act(o, ind(win, off))
+                kk = [k for k in range(16) if k != t]
+                for j in range(4):
+                    ks = kk[4 * j:4 * j + 4]
+                    rk = {k: sl(sg[h][i], k, NB, 16) for k in ks}
+                    if mode[i] == "2":
+                        for k in ks:
+                            o = sl(sm[h][i], HQ * k, HQ * k + HQ); tt(o, rk[k], zp, ALU.max); rk[k] = o
+                    if mode[i] == "3":
+                        p = ps(); o = sl(sm[h][i], 448 * j, 448 * j + HQ * len(ks))
+                        mm([m for a, k in enumerate(ks) for m in grp(sl(p, HQ * a, HQ * a + HQ), [(Ib, rk[k]), (nIb, zh)])])
+                        act(o, sl(p, 0, HQ * len(ks)), ACT.Relu)
+                        rk = {k: sl(o, HQ * a, HQ * a + HQ) for a, k in enumerate(ks)}
+                    mm(grp(G, [(Ws[k], rk[k]) for k in ks], first[0], False)); first[0] = False
+            tag[0] = "e%d%d" % (t, h)
+            eh, el = tile("bf", HQ), tile("bf", HQ)
+            tt(eh, ind(sl(H, 0, V), vnh), zh, ALU.max); tt(el, ind(sl(Lw, 0, V), vnh), zh, ALU.max)
+            mm(grp(G, [(Wb[t], eh), (nWb[t], el)], False, False))
+            ad = tile("bf", HQ); act(ad, d, ACT.Abs)
+            p = sl(ps(), 0, HQ); mm(grp(p, [(Bb, ad)]))
+            lk = tile("bf", HQ); ts(lk, p, TH + 0.5, ALU.is_lt)
+            mm(grp(G, [(nI4k, lk)], False, True))
+            p = sl(ps(), 0, HQ); mm(grp(p, [(I2, zh), (Ib, d)]))
+            r1 = tile("f32", HQ); hv = tile("bf", HQ); act(r1, p, None, MAGIC, 0.4995); act(hv, r1, None, -MAGIC)
+            p = sl(ps(), 0, HQ); mm(grp(p, [(Ih, mid), (Wt, hv)]))
+            r2 = tile("f32", HQ); qv = tile("bf", HQ); act(r2, p, None, MAGIC, 1.0 / V); act(qv, r2, None, -MAGIC)
+            p = ps(); pa, pb = sl(p, 0, HQ), sl(p, HQ, 2 * HQ)
+            mm(grp(pb, [(Ib, ad), (nIb, hv)]) + grp(pa, [(Bh, vw), (nWt, hv), (I2k, qv)]))
+            s2 = tile("hf", HQ); s3 = tile("bf", HQ); tt(s2, pa, lk, ALU.mult); tt(s3, pb, lk, ALU.mult)
+            p = ps(); pa, pb = sl(p, 0, HQ), sl(p, HQ, 2 * HQ)
+            mm(grp(pb, [(Ib, zh), (nIb, hv)]) + grp(pa, [(Wt, hv), (nI2k, qv), (Ih, s2)]))
+            zd = tile("bf", HQ); act(sl(M, V + q0, V + q0 + HQ), pa); act(zd, pb)
+            Lf = tile("hf", HQ); cp(Lf, Lh)
+            fa = tile("bf", HQ)
+            if cfg["faa"]: act(fa, G, ACT.Sign, -0.5 - TAU[t])
+            else: ts(fa, G, TAU[t] + 0.5, ALU.is_gt)
+            p = ps(); pa, pb = sl(p, 0, HQ), sl(p, HQ, 2 * HQ)
+            mm(grp(pb, [(Ih, Lf), (Wh[t], vw), (nIh, qr)])); mm(grp(pa, [(Tri, fa)]))
+            ov = tile("hf", 2 * HQ); oh, vc = sl(ov, 0, HQ), sl(ov, HQ, 2 * HQ)
+            ts(oh, pa, kf if cfg["faa"] else 0.5, ALU.is_gt); tt(vc, pb, oh, ALU.mult)
+            p = sl(ps(), 0, 14); nc = tile("f32", 8)
+            mm(grp(p, [(Ih, Qlist[h])], True, False) + relist(p, Wh, ov, 2 * HQ, False, True))
+            ts(sl(nc, 0, 7), sl(p, 0, 7), -float(V), ALU.mult, float(V), ALU.add); tt(sl(uf[h], 0, 7), sl(p, 7, 14), sl(nc, 0, 7), ALU.add)
+            uh = sl(ue, 8 * h, 8 * h + 7); cp(uh, sl(uf[h], 0, 7))
+            muh = sl(mu, q0, q0 + HQ); ts(muh, ind(sl(M, 0, V + q0 + HQ), uh), m012, ALU.mult)
+            if last:
+                p = sl(ps(), 0, 7)
+                mm(grp(p, [(W0[m], sl(muh, 7 * m, 7 * m + 7)) for m in range(16)])); act(sl(fin[h], 224, 231), p)
+            elif cfg["rl3"]:
+                for j in range(3): ts(sl(m3[h], 128 * j, 128 * j + HQ), muh, ke[j], ALU.mult)
+                p = sl(ps(), 0, 23); mm(relist(p, Wh, m3[h], 256 + HQ))
+                cp(sl(vl[t + 1], 8 * h, 8 * h + 7), sl(p, 0, 7)); cp(sl(nls[h], 0, 15), sl(p, 8, 23))
+            else:
+                p = sl(ps(), 0, 7); mm(relist(p, W0, muh, HQ)); cp(sl(vl[t + 1], 8 * h, 8 * h + 7), p)
+            p = ps(); pa, pb = sl(p, 0, HQ), sl(p, HQ, 2 * HQ)
+            mm(grp(pb, [(Bh, oh)])); s4 = tile("bf", HQ); tt(s4, pb, zd, ALU.mult)
+            mm(grp(pa, [(nIh, qr), (R0, muh)])); oa = tile("hf", HQ); tt(oa, pa, oh, ALU.mult)
+            p = sl(ps(), 0, HQ); mm(grp(p, [(Ib, hv), (Ib, s3), (Ib, s4)]))
+            act(sl(fin[h], HQ, 2 * HQ) if last else sl(z[t + 1], q0, q0 + HQ), p)
+            p = sl(ps(), 0, HQ); mm(grp(p, [(Ih, Lf), (Wh[t], vw), (nIh, vc), (Ih, oa)]))
+            if last:
+                act(sl(fin[h], 0, HQ), p)
+                send([(sl(fin[h], 0, 231), sl(finl[h], 0, 231))], 800)
+                cs = slice(q0, q0 + HQ)
+                dma("S", dram("yl", (A_, cs)), sl(finl[h], 0, HQ), 2200)
+                dma("S", dram("yz", (A_, cs)), sl(finl[h], HQ, 2 * HQ), 2200)
+                dma("S", dram("yv", (A_, cs)), sl(finl[h], 224, 231), 2200)
+            else:
+                ts(sl(Lo_[t + 1], q0, q0 + HQ), p, kn[t + 1], ALU.mult)
+                send([(sl(z[t + 1], q0, q0 + HQ), sl(zs[t + 1], q0, q0 + HQ)), (sl(Lo_[t + 1], q0, q0 + HQ), sl(Ls[t + 1], q0, q0 + HQ))], 500)
+            tag[0] = "u%d%d" % (t, h)
+            p = sl(ps(), 0, HQ); mm(grp(p, [(Ih, TriQ[h]), (nDB, oh), (Bh, vc)]))
+            act(sl(ubc, q0, q0 + HQ), p, None, float(V))
+        news = []
+        for h in range(2):
+            q0 = HQ * h; tag[0] = "u%d%d" % (t, h)
+            eq = tile("bf", HQ); tt(eq, ind(sl(uf[h], 0, 7), obc), sl(ubc, q0, q0 + HQ), ALU.is_equal)
+            dup = tile("bf", HQ); scan(dup, rzero, eq, ALU.mult, ALU.max)
+            o1 = tile("f32", 8); o2 = tile("f32", 8); so = tile("u16", 16)
+            if cfg["tia"]: act(sl(o1, 0, 7), sl(dup, 15, HQ, 16), None, 0.0, spare)
+            else: ts(sl(o1, 0, 7), sl(dup, 15, HQ, 16), spare, ALU.mult)
+            tt(sl(o2, 0, 7), sl(o1, 0, 7), sl(uf[h], 0, 7), ALU.max)
+            cp(sl(so, 0, 14, 2), sl(o2, 0, 7))
+            m32 = tile("f32", HQ); mn = tile("f32", HQ); hn, ln = tile("bf", HQ), tile("bf", HQ)
+            act(m32, ind(sl(M, 0, V + q0 + HQ), sl(ue, 8 * h, 8 * h + 7)))
+            p = sl(ps(), 0, HQ); mm(grp(p, [(Tm, m32)])); act(mn, p, None, ke[4])
+            if not last:
+                nl = nls[h]
+                if not cfg["rl3"]:
+                    for j in (1, 2): ts(sl(m3[h], 128 * j, 128 * j + HQ), sl(mu, q0, q0 + HQ), ke[j], ALU.mult)
+                    p = sl(ps(), 0, 15); mm(relist(p, Wh, sl(m3[h], 128, 384), 128 + HQ)); cp(sl(nl, 0, 15), p)
+                xa = tile("bf", HQ); act(xa, ind(X, sl(nl, 0, 7)))
+                tt(hn, ind(X, sl(nl, 8, 15)), xa, ALU.max); tt(ln, ind(X, sl(nl, 8, 15)), xa, ALU.min)
+            news.append((so, mn, hn, ln))
+        for h, (so, mn, hn, ln) in enumerate(news):
+            for tab, src, nm in ((M, mn, "m"),) if last else ((H, hn, "u"), (Lw, ln, "u"), (M, mn, "m")):
+                tag[0] = "%s%d%d" % (nm, t, h)
+                for b in range(7): cp(ind(tab, sl(so, 2 * b, 2 * b + 1)), sl(src, 16 * b, 16 * b + 16))
+    add("A", "dma", (dram("ya", (A_, A_)), ("rows", M, 6)), [sl(M, 0, V)], [], 60, 2400)
+
+    n = len(ops); eng = [o["eng"] for o in ops]; cost = [o["cost"] for o in ops]; lat = [o["lat"] for o in ops]
+    tls = [o["tiles"] for o in ops]; hop, peek = cfg["hop"], cfg["peek"]
+    pred = [[(j, cost[j] + lat[j] + (cfg["same"] if eng[j] == eng[i] else hop) if hard else 0.0) for j, hard in ops[i]["deps"].items()] for i in range(n)]
+    succ = [[] for _ in range(n)]
+    for i in range(n):
+        for j, w in pred[i]: succ[j].append((i, w))
+    back = [[(i, max(0.0, w - cost[j]) + cost[i] if w else 0.0) for i, w in succ[j]] for j in range(n)]
+    bsucc = [[] for _ in range(n)]
+    for j in range(n):
+        for i, w in back[j]: bsucc[i].append((j, w))
+    uses = {tl: len(set(a[0] for a in lst)) for tl, lst in psacc.items()}
+
+    def run(pr, pre_, suc_, av0):
+        left = dict(uses); bank, held, lastuse, bfree, extra = {}, [None] * 8, [[] for _ in range(8)], [0.0] * 8, []
+        miss = [len(x) for x in pre_]; st = [0.0] * n; av = list(av0); free = {e: 0.0 for e in "VAPGS"}; order = []
+        ready = [i for i in range(n) if miss[i] == 0]
+        while ready:
+            fb = [x for x in range(8) if held[x] is None]; b0 = min(fb, key=lambda x: bfree[x]) if fb else None
+            cand = []; s0 = 1e18; e0 = None
+            for i in ready:
+                s = max(av[i], free[eng[i]]); new = bool(tls[i]) and any(tl not in bank for tl in tls[i])
+                if new:
+                    if b0 is None: continue
+                    s = max(s, bfree[b0])
+                cand.append((s, i, new))
+                if s < s0: s0, e0 = s, eng[i]
+            if not cand: return None
+            s, i, new = max([c for c in cand if eng[c[1]] == e0 and c[0] <= s0 + peek], key=lambda c: pr[c[1]])
+            if new:
+                tl = [x for x in tls[i] if x not in bank][0]; bank[tl] = b0; held[b0] = tl
+                extra += [(i, j) for j in lastuse[b0]]; lastuse[b0] = []
+            for tl in tls[i]:
+                b = bank[tl]; lastuse[b].append(i); left[tl] -= 1; bfree[b] = max(bfree[b], s + cost[i] + lat[i] + hop)
+                if left[tl] == 0: held[b] = None
+            st[i] = s; free[eng[i]] = s + cost[i]; order.append(i); ready.remove(i)
+            for j, w in suc_[i]:
+                if s + w > av[j]: av[j] = s + w
+                miss[j] -= 1
+                if miss[j] == 0: ready.append(j)
+        return max(st[i] + cost[i] + lat[i] for i in range(n)), st, order, bank, extra
+    pr = [0.0] * n
+    for i in range(n - 1, -1, -1): pr[i] = max([pr[j] + w for j, w in succ[i]] + [cost[i] + lat[i]])
+    pr = [x + cfg["bias"].get(o["tag"], 0.0) for x, o in zip(pr, ops)]
+    best = run(pr, pred, succ, [0.0] * n); cur = best; rnd = [cfg["seed"]]
+    tags = sorted(set(o["tag"] + o["eng"] for o in ops))
+
+    def draw():
+        rnd[0] = (rnd[0] * 6364136223846793005 + 1442695040888963407) % 2 ** 64
+        return (rnd[0] >> 33) / 2.0 ** 31
+    for it in range(cfg["rounds"]):
+        amp = 3000.0 * draw() ** 2; nz = {tg: amp * (draw() - 0.5) for tg in tags}
+        r = run([cur[1][i] + cost[i] + nz[ops[i]["tag"] + eng[i]] for i in range(n)], back, bsucc, lat) if cur else None
+        f = run([r[1][i] + cost[i] for i in range(n)], pred, succ, [0.0] * n) if r else None
+        if f and (best is None or f[0] < best[0]): best = f
+        cur = f if f and f[0] < best[0] * 1.02 else best
+    _, st_t, order, bank, extra = best
+    fin_t = [st_t[i] + cost[i] + lat[i] for i in range(n)]
+    for i, j in extra: ops[i]["deps"][j] = ops[i]["deps"].get(j, False) or eng[j] != eng[i]
+
+    need = set(j for o in ops for j, hard in o["deps"].items() if hard)
+    cnt = {e: 0 for e in "VAPG"}; sig = {}; nd = [0]
+    for i in order:
+        o = ops[i]
+        if o["dma"]: sig[i] = ("d%d" % nd[0], 1); nd[0] += 1
+        elif i in need: cnt[o["eng"]] += 1; sig[i] = ("c" + o["eng"], cnt[o["eng"]])
+    know = {e: {} for e in "VAPGS"}; clock = {}; prog = []
+    for i in order:
+        o = ops[i]; kn_ = know[o["eng"]]; waits = []
+        for j in sorted([j for j, hard in o["deps"].items() if hard], key=lambda j: -fin_t[j]):
+            sname, val = sig[j]
+            if kn_.get(sname, 0) >= val: continue
+            waits.append(j)
+            for a, b in clock[j].items(): kn_[a] = max(kn_.get(a, 0), b)
+        if i in sig:
+            clock[i] = {} if o["kind"] == "send" else dict(kn_)
+            clock[i][sig[i][0]] = sig[i][1]
+        prog.append((o, [(sig[j], ops[j]) for j in waits], sig.get(i)))
+    return {"prog": prog, "bank": bank, "top": top, "cnt": cnt, "nd": nd[0], "end": max(fin_t), "ops": ops, "st": st_t, "fin": fin_t, "order": order, "pr": pr}
+
+
+PLAN = plan(CFG)
+SCRATCH = {"s_" + a: ("sbuf", [128, (PLAN["top"][a] + 15) // 16 * 16], DT[a]) for a in DT}
+SCRATCH.update({"ps%d" % b: ("psum", [128, 512], "float32") for b in range(8)})
+SEMAPHORES = ["cV", "cA", "cP", "cG", "sent"] + ["d%d" % i for i in range(PLAN["nd"])]
+
+
+def masks(topo, src, dst, n):
+    e = topo.engines(src, dst); k = len(e) // n
+    return [sum(1 << x for x in e[k * j:k * j + k]) for j in range(n)], k
+
+
+def rank_program(g, core, T, topo):
+    rank = T.rank_of(core)
+    if rank is None:
+        return
+    N = len(T.cores); nxt = T.cores[(rank + 1) % N]; prv = T.cores[(rank - 1) % N]
+    rid, pid = topo.addr(nxt, core)
+    Qs = {"V": g.vector, "A": g.scalar, "P": g.tensor, "G": g, "S": g.sync}
+
+    def ap(r):
+        if not isinstance(r, tuple): return r
+        if r[0] == "ind": return ap(r[1]).indirect(ap(r[2]))
+        if r[0] == "dram": return T[r[1]][r[2]]
+        if r[0] == "rows": return T["s_" + r[1][0]][r[2]:128:16, r[1][1]:r[1][1] + V]
+        buf = T["ps%d" % PLAN["bank"][r[5]]] if r[0] == "ps" else T["s_" + r[0]]
+        return buf[0:r[4], r[1]:r[2]] if r[3] == 1 else buf[0:r[4], r[1]:r[2]:r[3]]
+
+    def total(o):
+        if o["kind"] == "dma": return 16
+        return masks(topo, prv, core, len(o["args"]))[1] * len(o["args"])
+
+    sent = [0]; tail = []
+    for o, waits, sig in PLAN["prog"]:
+        q = Qs[o["eng"]]; a = o["args"]; k = o["kind"]
+        for (name, val), src in waits:
+            q.wait_ge(T.sem[name], total(src) if src["dma"] else val)
+        if k == "send":
+            ms, ne = masks(topo, core, nxt, len(a)); sent[0] += ne * len(a)
+            if len(a) == 1:
+                g.remote_dma(ap(a[0][1]), ap(a[0][0]), T.sem[sig[0]], T.sem.sent, pid, rid, ms[0])
+            else:
+                g.remote_dma_fused([RemoteDMATransfer(dst_ids=[DstId(rid=rid, pnc=pid)], dma_engine_mask=m, remote_sem=T.sem[sig[0]],
+                                                      src=ap(s), dst=ap(d)) for m, (s, d) in zip(ms, a)], local_sem=T.sem.sent)
+            tail.append((sig[0], total(o)))
+            continue
+        if k == "dma":
+            q.dma_start(ap(a[0]), ap(a[1])).then_inc(T.sem[sig[0]], 16); tail.append((sig[0], 16))
+            continue
+        if k == "cp": ins = q.tensor_copy(ap(a[0]), ap(a[1]))
+        elif k == "tt": ins = q.tensor_tensor(ap(a[0]), ap(a[1]), ap(a[2]), a[3])
+        elif k == "ts":
+            ins = q.tensor_scalar(ap(a[0]), ap(a[1]), ap(a[2]), None, a[4]) if a[5] is None else \
+                q.tensor_scalar(ap(a[0]), ap(a[1]), ap(a[2]), ap(a[3]), a[4], a[5])
+        elif k == "scan": ins = q.tensor_tensor_scan(ap(a[0]), ap(a[1]), ap(a[2]), 0.0, a[3], a[4])
+        elif k == "mset": ins = q.memset(ap(a[0]), a[1])
+        elif k == "act": ins = q.activation(ap(a[0]), ap(a[1]), a[2], bias=ap(a[3]), scale=ap(a[4]))
+        elif k == "asel": ins = q.affine_select(ap(a[0]), ap(a[1]), a[2], a[3], a[4], a[5], a[6])
+        elif k == "iota":
+            ins = q.iota(ap(a[0]), a[1], a[2], a[3]) if a[0][0] == "i32" else q.iota(ap(a[0]), a[1], a[2], a[3], allow_small_or_imprecise_dtypes=True)
+        else:
+            for m in a: ins = q.matmul(ap(m[0]), ap(m[1]), ap(m[2]), m[3], m[4])
+        if sig: ins.then_inc(T.sem[sig[0]], 1)
+    for e in "VAPG":
+        if PLAN["cnt"][e]: g.wait_ge(T.sem["c" + e], PLAN["cnt"][e])
+    g.wait_ge(T.sem.sent, sent[0])
+    for name, val in tail: g.wait_ge(T.sem[name], val)

@@ -3,23 +3,33 @@ from concourse.mybir import AluOpType, ActivationFunctionType
 
 ALU = AluOpType
 ACT = ActivationFunctionType
-V, Q, NV, HQ = 2048, 224, 3, 112
+V, Q, NV = 2048, 224, 3
 TH, TAU = 1020, (1020, 1530, 1275)
 MAGIC = 12582912.0
 BIG = 4194304.0
+TW = V + 32
+CQ = 32
 
 CFG = {
-    "wmode": ["ha", "ha", "ha"],
-    "smode": ["1123", "1123", "1123"],
-    "bias": {}, "seed": 1, "rounds": 150, "rl3": False, "faa": True, "kca": False, "tia": True, "zg": [16, 16, 16], "cs": 28, "cw": 28, "xav": 3,
-    "pe": 0.55, "hop": 110.0, "same": 70.0, "gat": 1.6, "sca": 3.9, "link": 2600.0, "peek": 30.0,
+    "segs": [(0, 128), (128, 224)], "esegs": [(0, 128), (128, 224)], "usegs": [(0, 128), (128, 224)],
+    "late": ["00", "00", "00"],
+    "wmode": ["aaaaaaa", "aaaaaaa", "aaaaaaa"],
+    "hmode": ["vvavvav", "vvavvav", "vvavvav"],
+    "lmode": ["vvavvav", "vvavvav", "vvavvav"],
+    "zg": [[12, 12], [12, 12], [12, 12]], "t1a": False, "ulast": True,
+    "sT": True, "rl": "pvp", "ne": 2, "xat": 1, "nr": 2,
+    "zl": False, "mum": False, "hva": False,
+    "seed": 2, "rounds": 600, "temp": 800.0, "pback": 0.4, "pflip": 0.25, "polish": 11000, "temp2": 150.0, "even": 0.1, "bb": 12, "peek": 30.0,
+    "cases": [(1.0, 1.6, 3.9, 0.55, 300.0, 1.0, 2600.0, 110.0, 70.0, 90000.0),
+              (0.9, 1.25, 2.8, 0.48, 500.0, 1.0, 3300.0, 110.0, 70.0, 86000.0),
+              (1.2, 2.2, 5.5, 0.65, 300.0, 1.1, 2600.0, 130.0, 80.0, 112000.0)],
 }
 DT = {"bf": "bfloat16", "hf": "float16", "f32": "float32", "i32": "int32", "u16": "uint16"}
 
 
 def plan(cfg):
     ops, top, acc, psacc = [], {a: 0 for a in DT}, {a: [] for a in DT}, {}
-    nps = [0]; tag = ["i"]
+    nps = [0]; tag = ["i"]; dry = []
     w2 = {"bf": True, "hf": True, "f32": False, "i32": False, "u16": True, "ps": False}
 
     def tile(a, n):
@@ -44,7 +54,14 @@ def plan(cfg):
     def isref(x):
         return isinstance(x, tuple)
 
-    def add(eng, kind, args, rd, wr, cost, lat=0.0):
+    def either(*ways):
+        dry.append([])
+        for f in ways: f()
+        got = dry.pop()
+        add(got[0][0], got[0][1], got[0][2], [r for x in got for r in x[4]], got[0][5], got[0][3], alts=[x[:4] for x in got])
+
+    def add(eng, kind, args, rd, wr, cost, lat=(0.0, 0.0), alts=None):
+        if dry: return dry[-1].append((eng, kind, args, cost, rd, wr))
         me = len(ops); deps = {}
         rr, ww = [], []
         for r in rd:
@@ -62,7 +79,7 @@ def plan(cfg):
                     tiles.append(r[5])
                     for o, ow, lo, hi in psacc.setdefault(r[5], []):
                         if o == me: continue
-                        hard = ops[o]["eng"] != eng or (ow and not isw and lo < r[2] and r[1] < hi)
+                        hard = ops[o]["eng"] != eng or alts is not None or len(ops[o]["alts"]) > 1 or (ow and not isw and lo < r[2] and r[1] < hi)
                         deps[o] = deps.get(o, False) or hard
                     psacc[r[5]].append((me, isw, r[1], r[2]))
                     continue
@@ -74,13 +91,13 @@ def plan(cfg):
                         if isw and r[3] == 1 and r[4] == 128 and r[1] <= lo and hi <= r[2]: continue
                     keep.append(e)
                 acc[r[0]] = keep + [(me, isw, r[1], r[2], r[3])]
-        ops.append({"eng": eng, "kind": kind, "args": args, "deps": deps, "cost": cost, "lat": lat, "dma": dma,
+        ops.append({"eng": eng, "deps": deps, "lat": lat, "dma": dma, "alts": alts or [(eng, kind, args, cost)],
                     "tiles": sorted(set(tiles)), "tag": tag[0]})
 
     def vcost(out, ins, per):
-        if out[0] == "ind": return 50 + cfg["sca"] * wd(out)
-        if ins[0][0] == "ind": return 50 + cfg["gat"] * wd(out)
-        return max(64.0, per * wd(ins[0])) + 10
+        if out[0] == "ind": return (50, 0, wd(out))
+        if ins[0][0] == "ind": return (50, wd(out))
+        return (max(64.0, per * wd(ins[0])) + 10,)
 
     def cp(out, i):
         add("V", "cp", (out, i), [i], [out], vcost(out, [i], 0.5 if i[0] != "ind" and out[0] != "ind" and w2[i[0]] and w2[out[0]] else 1))
@@ -96,369 +113,546 @@ def plan(cfg):
         add("V", "scan", (out, d0, d1, op0, op1), [d0, d1], [out], vcost(out, [d0], 0.5 if w2[d0[0]] and w2[d1[0]] and w2[out[0]] else 1))
 
     def mset(out, c):
-        add("V", "mset", (out, c), [], [out], max(64, wd(out)))
+        add("V", "mset", (out, c), [], [out], (max(64, wd(out)),))
 
     def act(out, i, f=None, bias=0.0, scale=1.0):
         add("A", "act", (out, i, f or ACT.Identity, bias, scale), [i] + [s for s in (bias, scale) if isref(s)], [out],
-            65 + cfg["gat"] * wd(out) if i[0] == "ind" else max(64, wd(out)) + 30)
+            (65, wd(out)) if i[0] == "ind" else (max(64, wd(out)) + 30,))
 
     def mm(lst):
-        c = sum(max(min(64, wd(m[1])), wd(m[2])) * (1 if w2[m[2][0]] else 4) * cfg["pe"] + 4 for m in lst)
-        add("P", "mm", lst, [m[1] for m in lst] + [m[2] for m in lst], [m[0] for m in lst], c, 60.0)
+        c = sum(max(min(64, wd(m[1])), wd(m[2])) * (1 if w2[m[2][0]] else 4) for m in lst)
+        add("P", "mm", lst, [m[1] for m in lst] + [m[2] for m in lst], [m[0] for m in lst], (4 * len(lst), 0, 0, c), (60.0, 0.0))
+
+    def move(out, i, first="A"):
+        either(*[lambda: act(out, i), lambda: cp(out, i)][::1 if first in "Aa" else -1])
+
+    def lin(out, i, scale, bias, first="A"):
+        either(*[lambda: act(out, i, None, bias, scale), lambda: ts(out, i, scale, ALU.mult, bias, ALU.add)][::1 if first == "A" else -1])
+
+    def relu(out, i):
+        either(lambda: act(out, i, ACT.Relu), lambda: ts(out, i, 0.0, ALU.max))
 
     def grp(out, pairs, start=True, stop=True):
         return [(out, a, b, start and j == 0, stop and j == len(pairs) - 1) for j, (a, b) in enumerate(pairs)]
 
-    def relist(out, W, src, n, start=True, stop=True):
-        return grp(out, [(W[m], sl(src, m, n, 16)) for m in range(16)], start, stop)
+    def relist(out, W, src, start=True, stop=True):
+        return grp(out, [(W[m], sl(src, m, wd(src), 16)) for m in range(16)], start, stop)
 
     def iota(out, pat, base=0, cm=0):
-        add("G", "iota", (out, pat, base, cm), [], [out], 130 + 2 * wd(out))
+        add("G", "iota", (out, pat, base, cm), [], [out], (130 + 2 * wd(out),))
 
     def asel(out, i, pat, op, fill, base, cm):
-        add("G", "asel", (out, i, pat, op, fill, base, cm), [i], [out], 170 + 2 * wd(out))
+        add("G", "asel", (out, i, pat, op, fill, base, cm), [i], [out], (170 + 2 * wd(out),))
 
     def spread(dst, src, on_g):
+        n = wd(src)
         for k in range(16):
-            if k < on_g: asel(sl(dst, k, 16 * HQ, 16), src, [[0, HQ]], ALU.is_gt, 0.0, 1, 0)
-            else: cp(sl(dst, k, 16 * HQ, 16), src)
+            o = sl(dst, k, 16 * n, 16)
+            either(*[lambda: asel(o, src, [[0, n]], ALU.is_gt, 0.0, 1, 0), lambda: cp(o, src)][::1 if k < on_g else -1])
 
-    def dma(eng, out, i, lat):
-        add(eng, "dma", (out, i), [i], [out], 60, lat)
+    def dma(eng, out, i, lat, rd=None):
+        add(eng, "dma", (out, i), rd or [i], [out], (60,), (lat, 0.0))
 
     def send(pairs, by):
-        add("G", "send", pairs, [p[0] for p in pairs], [p[1] for p in pairs], 300, cfg["link"] + by)
+        add("G", "send", pairs, [p[0] for p in pairs], [p[1] for p in pairs], (0, 0, 0, 0, 1), (0.0, 1.0 + by / 2600.0))
 
     def dram(name, idx):
         return ("dram", name, idx)
 
-    A_ = slice(None)
+    A_ = slice(None); segs, esegs, usegs = cfg["segs"], cfg["esegs"], cfg["usegs"]; F = float(V)
+    late = [[c == "1" for c in s] for s in cfg["late"]]
+    S = 128 if max(b - a for a, b in esegs) <= 128 else 256
+
+    def inside(a, b, parts):
+        return [(h, x, y) for h, (x, y) in enumerate(parts) if a <= x and y <= b]
     E = tile("i32", V); X = tile("bf", V); v0 = tile("i32", 16); L0 = tile("i32", Q)
     z = [tile("bf", Q) for _ in range(NV)]
     dma("A", sl(v0, 0, 14), dram("v0", (A_, A_)), 2000)
-    for j in range(2):
-        dma("S", sl(E, 1024 * j, 1024 * j + 1024), dram("E", (A_, slice(1024 * j, 1024 * j + 1024))), 3600 + 1800 * j)
+    ne = cfg["ne"]; ce = V // ne; at = 2000
+    for j in range(ne + 1):
+        if j == cfg["xat"]:
+            at += 1700; dma("S", X, dram("X", (A_, A_)), at)
+        if j < ne:
+            at += 3400 // ne; dma("S", sl(E, ce * j, ce * j + ce), dram("E", (A_, slice(ce * j, ce * j + ce))), at)
     dma("A", z[0], dram("z0", (A_, A_)), 2300)
     dma("A", L0, dram("L0", (A_, A_)), 2600)
-    dma("S", X, dram("X", (A_, A_)), 7000)
 
     pi = tile("i32", 16); iota(sl(pi, 0, 1), [[0, 1]], 0, 1)
-    col = tile("f32", Q); iota(col, [[1, Q]])
+    col = tile("f32", 160); iota(col, [[1, 160]])
     colk = tile("f32", 128); iota(colk, [[0, 8], [1, 16]])
     colg = tile("f32", 128); iota(colg, [[16, 8], [0, 16]])
-    oi = tile("i32", 16); iota(sl(oi, 0, 8), [[16, 8]], 15); iota(sl(oi, 8, 16), [[1, 8]])
-    ou = tile("u16", 16); cp(ou, oi)
-    olast, obc = sl(ou, 0, 8), sl(ou, 8, 15)
+    oi = tile("i32", 16); iota(sl(oi, 0, 8), [[1, 8]])
+    olast = sl(tile("u16", 16), 0, 8); cp(olast, sl(oi, 0, 8))
     C = tile("f32", 32)
     cc = [sl(C, j, j + 1) for j in range(32)]
-    ki = tile("i32", 16); ts(sl(ki, 0, 1), sl(pi, 0, 1), 15, ALU.bitwise_and)
+    ki = tile("i32", 16); ts(sl(ki, 0, 1), sl(pi, 0, 1), 15, ALU.bitwise_and); ts(sl(ki, 1, 2), sl(pi, 0, 1), 1, ALU.bitwise_and)
     pf, kf, gb = cc[0], cc[1], cc[2]
     cp(pf, sl(pi, 0, 1)); cp(kf, sl(ki, 0, 1)); tt(gb, pf, kf, ALU.subtract)
     KE = tile("f32", 16); ts(KE, sl(col, 0, 16), kf, ALU.is_equal)
     KN = tile("f32", 16); ts(KN, sl(col, 0, 16), kf, ALU.not_equal)
     ke = [sl(KE, j, j + 1) for j in range(16)]; kn = [sl(KN, j, j + 1) for j in range(16)]
-    c128 = sl(col, 0, 128); k112 = sl(colk, 0, HQ)
 
-    def times(src, s):
-        t = tile("bf", wd(src)); act(t, src, None, 0.0, s); return t
+    def times(src, s, a="bf"):
+        t = tile(a, wd(src)); lin(t, src, s, 0.0); return t
+
+    def timev(src, s, s2=None):
+        if s2 is None: return times(src, s)
+        t = tile("bf", wd(src)); ts(t, src, s, ALU.mult, s2, ALU.mult); return t
 
     def cuts(t):
         return [sl(t, 15 - m, 143 - m) for m in range(16)]
 
     def summed(a, parts):
         p = sl(ps(), 0, 128); mm(grp(p, [(Ib, x) for x in parts])); t = tile(a, 128); act(t, p); return t
-    p8, g15 = cc[20], cc[3]; ts(p8, pf, 8.0, ALU.add); ts(g15, gb, 15.0, ALU.add)
-    Iw = tile("bf", 144); ts(Iw, sl(col, 0, 144), p8, ALU.is_equal)
-    Ib = Ih = sl(Iw, 8, 136); J = sl(Iw, 12, 140)
-    nIb, I2, I2k, nI2k, nI4k = [times(Ib, s) for s in (-1.0, 2.0, 2048.0, -2048.0, -4096.0)]
-    nIh = nIb
+    p16, g15 = cc[20], cc[3]; ts(p16, pf, 16.0, ALU.add); ts(g15, gb, 15.0, ALU.add)
+    Iw = tile("bf", 160); ts(Iw, col, p16, ALU.is_equal)
+    down = [sl(Iw, 16 + m, 144 + m) for m in range(16)]
+    Ib = down[0]; J = down[4]
+    nIb, Ihalf, IrS, Ir8k = [timev(Ib, s) for s in (-1.0, 0.5, 1.0 / S, 1 / 8192.0)]
+    if cfg["t1a"] or "a" in cfg["rl"]: I32 = times(Ib, 1.0, "f32")
     Ww = tile("bf", 144); ts(Ww, sl(col, 0, 144), g15, ALU.is_equal)
-    Wb = Wh = cuts(Ww); nWb, W0, W1 = cuts(times(Ww, -1.0)), cuts(times(Ww, ke[0])), cuts(times(Ww, ke[1]))
-    wt, nwt, k1 = cc[4], cc[5], cc[6]
-    ts(wt, kf, 2.0, ALU.mult, 1.0, ALU.add); ts(nwt, kf, -2.0, ALU.mult, -1.0, ALU.add); ts(k1, kf, 1.0, ALU.add)
-    Bb = Bh = tile("bf", 128); ts(Bb, colg, gb, ALU.is_equal)
-    nBb, nDB, R0, Wt, nWt = [times(Bb, s) for s in (-1.0, -2048.0, ke[0], wt, nwt)]
-    G32 = times(sl(Bb, 0, 128, 16), 32.0)
-    G64, nG32 = (times(G32, 2.0), times(G32, -1.0)) if any("m" in s for s in cfg["wmode"]) else (None, None)
-    Kc = tile("bf", HQ); act(Kc, k112, None, kf, 0.0)
+    wt, k1 = cc[4], cc[6]
+    ts(wt, kf, 2.0, ALU.mult, 1.0, ALU.add); ts(k1, kf, 1.0, ALU.add)
+    Wb = cuts(Ww); W0, W1 = [cuts(times(Ww, s)) for s in (ke[0], ke[1])]
+    Bb = tile("bf", 128); ts(Bb, colg, gb, ALU.is_equal)
+    nBr, R0r, Br = times(Bb, -1.0 / S), timev(Bb, ke[0], 1.0 / S), times(Bb, 1.0 / S)
+    G8 = sl(Bb, 0, 128, 16); G32 = times(G8, 32.0)
+    anyl = any(any(x) for x in late)
+    sg_ = 1.0 / (8192 * S); Wt8, nG8s = timev(G8, wt, sg_), times(G8, -sg_); I16 = sl(Ib, 0, 16)
+    G80 = times(G8, ke[0]) if cfg["rl"][2] != "p" else None
+    nIq = timev(I16, -F * sg_); Icq = [timev(I16, -2.0 * c * F * sg_) for c in (160, 159)[:1 + anyl]]
+    nR8 = [timev(G8, ke[t], -sg_) if any(late[t]) else None for t in range(NV)]
+
+    def blocks(out, src, G, one=True):
+        return [(sl(out, m, 128, 16), sl(src, m, wd(src), 16), G, one, one) for m in range(16)]
+
+    def tolist(out, src, W, G, how, stop=False):
+        if how == "p": return relist(out, W, src, True, stop)
+        k = wd(out); p = sl(ps(), 0, 128, 1, k); mm(blocks(p, src, G))
+        u = sl(tile("f32" if how == "a" else "hf", 128), 0, 128, 1, k); (move if how == "a" else cp)(u, p)
+        return [(out, u, sl(I32 if how == "a" else Ib, 0, k, 1, k), True, stop)]
+    if cfg["sT"]: nG8 = times(G8, -1.0)
+    else: nWb = cuts(times(Ww, -1.0)); nBb = times(Bb, -1.0)
+    Kc = tile("bf", 128); act(Kc, colk, None, kf, 0.0)
+    nK0 = timev(Ib, ke[0], -2.0); cq = tile("bf", Q); mset(cq, -0.5)
     rbig = tile("f32", 128); ts(rbig, colk, 0.0, ALU.is_equal, BIG, ALU.mult)
-    rzero = tile("bf", HQ); act(rzero, k112, ACT.Sign)
-    Tri = tile("bf", 128); tmpa = tile("bf", 128)
-    asel(tmpa, nBb, [[1, 128]], ALU.is_gt, 0.0, 0, -1); asel(Tri, tmpa, [[1, 128]], ALU.not_equal, 1.0, 0, -1)
-    TriD = tile("hf", HQ); ts(TriD, k112, kf, ALU.is_ge, 0.5, ALU.mult)
-    Qrow = tile("bf", Q); act(Qrow, col)
-    TriQ = [tile("hf", HQ) for _ in range(2)]; Qlist = [sl(tile("bf", 16), 0, 14) for _ in range(2)]
-    m3 = [tile("hf", 384) for _ in range(2)]
-    for h in range(2):
-        tt(TriQ[h], sl(Qrow, HQ * h, HQ * h + HQ), TriD, ALU.add)
-        act(sl(Qlist[h], 0, 7), sl(col, 0, 7), None, 0.0, 0.0); act(sl(Qlist[h], 7, 14), sl(col, 7 * h, 7 * h + 7), None, kf, 16.0)
-        for j in range(2): ts(sl(m3[h], 128 * j + HQ, 128 * j + 128), sl(col, 0, 16), 0.0, ALU.mult)
-    mid = tile("hf", HQ); ts(mid, k112, 0.0, ALU.mult, 0.5 - V // 2, ALU.add)
-    m012, m16, spare, m03 = cc[7], cc[8], cc[10], cc[11]
-    ts(m012, kf, 2.5, ALU.is_lt); ts(m03, kf, 3.5, ALU.is_lt)
-    tt(cc[12], ke[4], ke[5], ALU.add); ts(m16, cc[12], 16.0, ALU.mult); ts(spare, kf, float(V + Q), ALU.add)
+    nu = max(b - a for a, b in usegs); rone = tile("bf", nu); TriD = tile("bf", nu); tri = tile("bf", 128)
+    ts(tri, colk, kf, ALU.is_ge, 4096.0 / S, ALU.mult)
+    for a in range(0, nu, 128):
+        b = min(nu, a + 128)
+        ts(sl(rone, a, b), sl(colk, 0, b - a), 0.0, ALU.is_equal)
+        asel(sl(TriD, a, b), sl(tri, 0, b - a), [[0, (b - a) // 16], [-1, 16]], ALU.not_equal, 0.0, 15, 0)
+    byB = cfg["rl"][1] == "v"; Rb = {}
+    for n in sorted(set(b - a for a, b in esegs)) if byB else []:
+        r0 = tile("bf", n); r1 = tile("f32", n); iota(r1, [[1, n // 16], [0, 16]], n // 16, -1)
+        ts(r0, r1, 0.0, ALU.is_equal, 1.0 / S, ALU.mult); Rb[n] = sl(tile("bf", n), 0, n, 1, n // 8)
+        asel(sl(Rb[n], 0, n, 1, 128), r0, [[0, n // 16], [-1, 16]], ALU.not_equal, 0.0, 15, 0)
+    T8 = tile("bf", 128); tmpa = tile("bf", 128)
+    asel(tmpa, times(Bb, -8192.0), [[1, 128]], ALU.is_gt, 0.0, 0, -1); asel(T8, tmpa, [[1, 128]], ALU.not_equal, 8192.0, 0, -1)
+    thr, qb = cc[21], cc[22]; ts(thr, kf, 8192.0, ALU.mult, 8192.0 + TH + 0.5, ALU.add); ts(qb, kf, -F, ALU.add)
+    Qlist = sl(tile("hf", 16), 0, 14); ts(Qlist, sl(col, 0, 14), 16.0, ALU.mult, qb, ALU.add)
+    m012, m16, spare, m03, m12, rTW = cc[7], cc[8], cc[10], cc[11], cc[23], cc[24]
+    ts(m012, kf, 2.5, ALU.is_lt); ts(m03, kf, 3.5, ALU.is_lt); tt(m12, m012, ke[0], ALU.subtract)
+    tt(cc[12], ke[4], ke[5], ALU.add); ts(m16, cc[12], 16.0, ALU.mult); ts(spare, kf, 1.0, ALU.add)
+    ts(rTW, sl(ki, 1, 2), float(TW), ALU.mult, F, ALU.add)
+    Vw = times(Iw, m12); pair = [sl(Vw, 17 - 2 * s, 145 - 2 * s) for s in range(8)]
+    colh = tile("f32", 128); iota(colh, [[16, 8], [1, 8], [0, 2]])
+    twice = [tile("bf", 128) for _ in range(2)]; ts(cc[25], pf, -8.0, ALU.add)
+    ts(twice[0], colh, pf, ALU.is_equal); ts(twice[1], colh, cc[25], ALU.is_equal)
     Mi = summed("bf", [times(Ib, m03), times(Wb[6], k1), Wb[7]])
     tt(cc[17], m03, ke[0], ALU.subtract); ts(cc[18], ke[0], 16.0, ALU.mult, ke[6], ALU.add); tt(cc[19], cc[18], ke[7], ALU.subtract)
-    Tm = summed("f32", [times(sl(Iw, 9, 137), cc[17]), times(sl(Iw, 7, 135), ke[4]), times(Wb[6], cc[19]), times(Wb[7], ke[7])])
-    pk = tile("f32", 512); iota(pk, [[0, 512]])
-    pre = [sl(pk, 128 * h, 128 * h + 128) for h in range(2)]; kc = [sl(pk, 256 + 128 * h, 384 + 128 * h) for h in range(2)]
+    Tm = summed("f32", [times(down[1], cc[17]), times(sl(Iw, 15, 143), ke[4]), times(Wb[6], cc[19]), times(Wb[7], ke[7])])
+    if anyl:
+        KF = tile("f32", 16); ts(KF, KN, F, ALU.mult); kF = [sl(KF, j, j + 1) for j in range(16)]
+    Ik = [times(Ib, kn[t]) if any(late[t]) else None for t in range(NV)]
+    nIk = [timev(Ib, kn[t], -1.0) if t and any(late[t]) else None for t in range(NV)]
+    Wr = [times(Wb[t], 1.0 / S) if not all(late[t]) else None for t in range(NV)]
+    pre = [tile("f32", 128) for _ in segs]; ge = [tile("bf", 144) for _ in segs]
+    for h in range(len(segs)):
+        mset(pre[h], 0.0); mset(sl(ge[h], 0, 16), 1.0)
+    Zw = [[tile("bf", 3 * S) for _ in esegs] for _ in range(NV)]
+    for t in range(NV):
+        for e, (a, b) in enumerate(esegs):
+            if b - a < S: mset(sl(Zw[t][e], b - a, S), 0.0); mset(sl(Zw[t][e], S + b - a, 2 * S), 0.0)
 
-    zs = [tile("bf", Q) for _ in range(NV)]; Ls = [tile("u16", Q) for _ in range(NV)]
+    def zland(t, a, b):
+        e = [e for e, (x, y) in enumerate(esegs) if x <= a and b <= y][0]
+        return sl(Zw[t][e], 2 * S + a - esegs[e][0], 2 * S + b - esegs[e][0])
+
+    Ls = [tile("u16", Q) for _ in range(NV)]
     Lo_ = [tile("u16", Q) for _ in range(NV)]
     vl = [tile("u16", 16) for _ in range(NV)]
-    ts(Lo_[0], L0, kn[0], ALU.mult)
-    send([(z[0], zs[0]), (Lo_[0], Ls[0])], 900)
-    for h in range(2): cp(sl(vl[0], 8 * h, 8 * h + 7), sl(v0, 7 * h, 7 * h + 7))
+    terms = {}
+    Lm0 = tile("hf", Q)
+    for h, (q0, q1) in enumerate(esegs):
+        zo = (sl(z[0], q0, q1), zland(0, q0, q1))
+        if late[0][h]:
+            ts(sl(Lm0, q0, q1), sl(L0, q0, q1), -F, ALU.add); terms[h] = [(1, sl(Lm0, q0, q1))]; send([zo], 300)
+        else:
+            ts(sl(Lo_[0], q0, q1), sl(L0, q0, q1), kn[0], ALU.mult)
+            send([zo, (sl(Lo_[0], q0, q1), sl(Ls[0], q0, q1))], 500)
+    cp(sl(vl[0], 0, 14), sl(v0, 0, 14))
 
     tag[0] = "t"
-    TW = V + Q + 16
-    M = tile("f32", TW); H = tile("bf", TW); Lw = tile("bf", TW); Ef = tile("hf", V); Xa = tile("bf", V)
+    M = tile("f32", TW); HL = tile("bf", 2 * TW); Ef = tile("hf", V); Xa = tile("bf", V)
+    H, Lw = sl(HL, 0, V), sl(HL, TW, TW + V); Mw = sl(M, 0, V + 16)
+    mset(sl(M, V, TW), 0.0)
     for j in range(4): cp(sl(Ef, 512 * j, 512 * j + 512), sl(E, 512 * j, 512 * j + 512))
-    ab = tile("u16", 256)
-    for j, Wj in enumerate((W0, W1)):
-        p = sl(ps(), 0, 128); mm(relist(p, Wj, Ef, V)); cp(sl(ab, 128 * j, 128 * j + 128), p)
+    ab = [tile("u16", 128) for _ in range(2)]; cr = V // cfg["nr"]
+    for i in range(cfg["nr"]):
+        for j, Wj in enumerate((W0, W1)):
+            p = sl(ps(), 0, cr // 16); mm(relist(p, Wj, sl(Ef, cr * i, cr * i + cr))); cp(sl(ab[j], cr // 16 * i, cr // 16 * (i + 1)), p)
     for j in range(4):
         c0, o0 = 512 * j, 32 * j
-        (cp if cfg.get("xav", 0) > j else act)(sl(Xa, c0, c0 + 512), ind(X, sl(ab, o0, o0 + 32)))
-        tt(sl(H, c0, c0 + 512), ind(X, sl(ab, 128 + o0, 160 + o0)), sl(Xa, c0, c0 + 512), ALU.max)
-        tt(sl(Lw, c0, c0 + 512), ind(X, sl(ab, 128 + o0, 160 + o0)), sl(Xa, c0, c0 + 512), ALU.min)
+        move(sl(Xa, c0, c0 + 512), ind(X, sl(ab[0], o0, o0 + 32)))
+        tt(sl(H, c0, c0 + 512), ind(X, sl(ab[1], o0, o0 + 32)), sl(Xa, c0, c0 + 512), ALU.max)
+        tt(sl(Lw, c0, c0 + 512), ind(X, sl(ab[1], o0, o0 + 32)), sl(Xa, c0, c0 + 512), ALU.min)
     tag[0] = "n"
     for j in range(4):
-        p = ps(); mm(grp(p, [(Mi, sl(Ef, 512 * j, 512 * j + 512))])); act(sl(M, 512 * j, 512 * j + 512), p)
-    NB = 16 * HQ
-    xg = [tile("bf", NB) for _ in range(2)]; xd = [tile("bf", NB) for _ in range(2)]
-    sg = [[tile("bf", NB) for _ in range(2)] for _ in range(2)]; sm = [[tile("bf", NB) for _ in range(2)] for _ in range(2)]
-    zr = [tile("bf", NB) for _ in range(2)]; zw = [tile("bf", NB) for _ in range(2)]
-    fin = [tile("f32", 240) for _ in range(2)]; finl = [tile("f32", 240) for _ in range(2)]
+        p = ps(); mm(grp(p, [(Mi, sl(Ef, 512 * j, 512 * j + 512))])); move(sl(M, 512 * j, 512 * j + 512), p)
+    NB = 16 * Q
+    fz = tile("bf", Q); fzl = tile("bf", Q); fin = [tile("f32", 2 * (b - a)) for a, b in esegs]; finl = [tile("f32", 2 * (b - a)) for a, b in esegs]
 
     for t in range(NV):
         last = t == NV - 1
-        vcl = tile("hf", Q); dl = tile("bf", Q); vnl = tile("u16", 16)
-        for h in range(2):
-            mode = cfg["wmode"][t][h]; tag[0] = "w%d%d" % (t, h)
-            zh = sl(z[t], HQ * h, HQ * h + HQ); vh = sl(vl[t], 8 * h, 8 * h + 7)
-            c = tile("u16", HQ); cp(c, ind(E, vh))
-            if mode == "z":
-                for k in range(16): cp(sl(zw[h], k, NB, 16), zh)
-            cq = cfg["cw"]
-            for j in range(HQ // cq):
-                c0, c1 = 16 * cq * j, 16 * cq * (j + 1)
-                o, src = sl(xg[h], c0, c1), ind(X, sl(c, cq * j, cq * (j + 1)))
-                if mode == "z":
-                    tt(o, src, sl(zw[h], c0, c1), ALU.subtract); act(sl(xd[h], c0, c1), o, ACT.Abs)
-                else: (cp if mode == "v" or (mode == "h" and j % 2) else act)(o, src)
-            ch = tile("hf", HQ); cp(ch, c)
-            key = sl(ps(), 0, 128, 1, HQ)
-            ko = [sl(key, k, 128, 16) for k in range(16)]
-            xk = [sl(xg[h], k, NB, 16) for k in range(16)]; dk = [sl(xd[h], HQ * k, HQ * k + HQ) for k in range(16)]
-            if mode == "m":
-                zp = sl(ps(), 0, HQ); mm(grp(zp, [(Ib, zh)]))
+        vcl = tile("hf", Q); xvl = tile("bf", Q); vnl = tile("u16", 16)
+        xg, xd, zr = tile("bf", NB), tile("bf", NB), tile("bf", NB); sg = [tile("bf", NB) for _ in range(2)]
+        for h, (q0, q1) in enumerate(segs):
+            n = q1 - q0; b0, b1 = q0 // 16, q1 // 16; nb = b1 - b0; tag[0] = "w%d%d" % (t, h)
+            zh = sl(z[t], q0, q1); vh = sl(vl[t], b0, b1)
+            c = tile("u16", n); cp(c, ind(E, vh))
+            for a in range(q0, q1, CQ):
+                move(sl(xg, 16 * a, 16 * a + 16 * CQ), ind(X, sl(c, a - q0, a - q0 + CQ)), cfg["wmode"][t][a // CQ])
+            ch = tile("hf", n); cp(ch, c)
+            key = sl(ps(), 0, 128, 1, n)
             for j in range(4):
-                ks = range(4 * j, 4 * j + 4)
-                head = [(key, Kc, Ib, True, False)] if j == 0 else []
-                end = t == 0 and j == 3
-                if mode == "m":
-                    for k in ks: tt(dk[k], xk[k], zp, ALU.max)
-                    mm(head + [m for k in ks for m in ((ko[k], xk[k], nG32, False, False), (ko[k], dk[k], G64, False, end and k == 15))])
-                elif mode == "z":
-                    mm(head + [(ko[k], sl(xd[h], k, NB, 16), G32, False, end and k == 15) for k in ks])
-                else:
-                    p = ps()
-                    mm([m for k in ks for m in grp(sl(p, HQ * (k % 4), HQ * (k % 4) + HQ), [(Ib, xk[k]), (nIb, zh)])])
-                    act(sl(xd[h], 448 * j, 448 * j + 448), sl(p, 0, 448), ACT.Abs)
-                    mm(head + [(ko[k], dk[k], G32, False, end and k == 15) for k in ks])
+                ks = range(4 * j, 4 * j + 4); p = ps(); o = 16 * q0 + 4 * n * j
+                mm([m for k in ks for m in grp(sl(p, n * (k % 4), n * (k % 4) + n), [(Ib, sl(xg, 16 * q0 + k, 16 * q1, 16)), (nIb, zh)])])
+                act(sl(xd, o, o + 4 * n), sl(p, 0, 4 * n), ACT.Abs)
+                mm(([(key, sl(Kc, 0, n), Ib, True, False)] if j == 0 else []) +
+                   [(sl(key, k, 128, 16), sl(xd, o + n * (k % 4), o + n * (k % 4) + n), G32, False, t == 0 and k == 15) for k in ks])
             tag[0] = "x%d%d" % (t, h)
             if t > 0:
-                fl = tile("bf", HQ); ts(fl, ind(sl(M, 0, V), vh), m16, ALU.mult)
+                fl = tile("bf", n); lin(fl, ind(Mw, vh), m16, 0.0)
                 mm([(key, fl, J, False, True)])
-            kch = sl(kc[h], 0, 128, 1, HQ)
-            if cfg["kca"]:
-                act(kch, key); scan(sl(pre[h], 0, 128, 1, HQ), sl(rbig, 0, 128, 1, HQ), kch, ALU.add, ALU.min)
-            else:
-                scan(sl(pre[h], 0, 128, 1, HQ), sl(rbig, 0, 128, 1, HQ), key, ALU.add, ALU.min); cp(kch, key)
-            hot = tile("hf", 128); tt(hot, ind(pre[h], olast), kc[h], ALU.is_equal)
-            oh = sl(ps(), 0, HQ); mm(grp(oh, [(sl(hot, 0, 128, 1, HQ), sl(Ih, 0, HQ, 1, HQ))]))
-            vc = tile("hf", HQ); tt(vc, oh, ch, ALU.mult)
-            p = sl(ps(), 0, 7); mm(relist(p, Wh, vc, HQ))
-            vn = tile("u16", 8); cp(sl(vn, 0, 7), p)
-            send([(sl(vn, 0, 7), sl(vnl, 8 * h, 8 * h + 7))], 0)
-            d = tile("bf", HQ); tt(d, ind(X, sl(vn, 0, 7)), zh, ALU.subtract)
-            send([(vc, sl(vcl, HQ * h, HQ * h + HQ)), (d, sl(dl, HQ * h, HQ * h + HQ))], 500)
-        ue = tile("u16", 16); uf = [tile("f32", 8) for _ in range(2)]; ubc = tile("f32", Q); mu = tile("hf", Q)
-        nls = [tile("u16", 16) for _ in range(2)]
-        for h in range(2):
-            mode = cfg["smode"][t][2 * h:2 * h + 2]; q0 = HQ * h; tag[0] = "s%d%d" % (t, h)
-            zh = sl(zs[t], q0, q0 + HQ); Lh = sl(Ls[t], q0, q0 + HQ); vw = sl(vcl, q0, q0 + HQ); d = sl(dl, q0, q0 + HQ)
-            vnh = sl(vnl, 8 * h, 8 * h + 7); qr = sl(Qrow, q0, q0 + HQ)
-            G = sl(ps(), 0, HQ); first = [True]
-            if "1" in mode:
-                spread(zr[h], zh, cfg["zg"][t])
-            if "2" in mode:
-                zp = sl(ps(), 0, HQ); mm(grp(zp, [(Ib, zh)]))
-            if mode.count("3") == 1:
-                mm(grp(G, [(Bb, zh), (nWb[t], zh)] if mode[0] == "3" else [(nBb, zh), (Wb[t], zh)], True, False)); first[0] = False
-            for i, (tab, Ws) in enumerate(((H, Wb), (Lw, nWb))):
-                win = sl(tab, 0, V)
-                cq = cfg["cs"]
-                for j in range(HQ // cq):
-                    o, off = sl(sg[h][i], 16 * cq * j, 16 * cq * (j + 1)), sl(Lh, cq * j, cq * (j + 1))
-                    if mode[i] == "1": tt(o, ind(win, off), sl(zr[h], 16 * cq * j, 16 * cq * (j + 1)), ALU.max)
-                    else: act(o, ind(win, off))
-                kk = [k for k in range(16) if k != t]
+            scan(sl(pre[h], 0, 128, 1, n), sl(rbig, 0, 128, 1, n), key, ALU.add, ALU.min)
+            least = tile("f32", 8); cp(least, sl(pre[h], 15, 128, 16))
+            tt(sl(ge[h], 16, 144), ind(least, olast), pre[h], ALU.is_equal)
+            oh = sl(ps(), 0, n)
+            mm(grp(oh, [(nK0, sl(cq, 0, n)), (sl(ge[h], 15, 143, 1, n), sl(nIb, 0, n, 1, n)), (sl(ge[h], 16, 144, 1, n), sl(Ib, 0, n, 1, n))]))
+            vc = tile("hf", n); tt(vc, oh, ch, ALU.mult)
+            if late[t][h]:
+                p = sl(ps(), 0, n); mm(grp(p, [((Ik[t] if s > 0 else nIk[t]), x) for s, x in terms[h]] + [(Wb[t], vc)]))
+                ts(sl(Lo_[t], q0, q1), p, kF[t], ALU.add)
+                send([(sl(Lo_[t], q0, q1), sl(Ls[t], q0, q1))], 300)
+            p = sl(ps(), 0, nb); mm(tolist(p, vc, Wb, G8, cfg["rl"][0], True))
+            vn = tile("u16", nb); cp(vn, p)
+            send([(vn, sl(vnl, b0, b1))], 0)
+            xv = tile("bf", n); move(xv, ind(X, vn))
+            send([(xv, sl(xvl, q0, q1))] + ([] if late[t][h] else [(vc, sl(vcl, q0, q1))]), 300 if late[t][h] else 500)
+        fa = tile("bf", Q)
+        for e, (a, b) in enumerate(esegs):
+            tag[0] = "z%d%d" % (t, e); spread(sl(zr, 16 * a, 16 * b), zland(t, a, b), cfg["zg"][t][e])
+        for h, (q0, q1) in enumerate(segs):
+            n = q1 - q0; b0, b1 = q0 // 16, q1 // 16; tag[0] = "s%d%d" % (t, h); lt = late[t][h]; sT = cfg["sT"]
+            zh = zland(t, q0, q1); vnh = sl(vnl, b0, b1); fix = []
+            kk = [k for k in range(16) if lt or k != t]
+            G = sl(ps(), 0, 128, 1, n) if sT else sl(ps(), 0, n)
+            for i, (win, md) in enumerate(((H, cfg["hmode"][t]), (Lw, cfg["lmode"][t]))):
+                for a in range(q0, q1, CQ):
+                    o, off, zz = sl(sg[i], 16 * a, 16 * a + 16 * CQ), sl(Ls[t], a, a + CQ), sl(zr, 16 * a, 16 * a + 16 * CQ)
+                    if md[a // CQ] == "v": tt(o, ind(win, off), zz, ALU.max)
+                    else:
+                        raw = tile("bf", 16 * CQ); act(raw, ind(win, off))
+                        p = sl(ps(), 0, 16 * CQ); mm(grp(p, [(nIb, zz), (Ib, raw)])); relu(o, p)
+                        if cfg["hmode"][t][a // CQ] != cfg["lmode"][t][a // CQ]:
+                            go, za = sl(G, a - q0, a - q0 + CQ), sl(zh, a - q0, a - q0 + CQ)
+                            fix += [(go, (Bb, nBb)[i], za, False, False)] + ([] if lt else [(go, (nWb, Wb)[i][t], za, False, False)])
                 for j in range(4):
-                    ks = kk[4 * j:4 * j + 4]
-                    rk = {k: sl(sg[h][i], k, NB, 16) for k in ks}
-                    if mode[i] == "2":
-                        for k in ks:
-                            o = sl(sm[h][i], HQ * k, HQ * k + HQ); tt(o, rk[k], zp, ALU.max); rk[k] = o
-                    if mode[i] == "3":
-                        p = ps(); o = sl(sm[h][i], 448 * j, 448 * j + HQ * len(ks))
-                        mm([m for a, k in enumerate(ks) for m in grp(sl(p, HQ * a, HQ * a + HQ), [(Ib, rk[k]), (nIb, zh)])])
-                        act(o, sl(p, 0, HQ * len(ks)), ACT.Relu)
-                        rk = {k: sl(o, HQ * a, HQ * a + HQ) for a, k in enumerate(ks)}
-                    mm(grp(G, [(Ws[k], rk[k]) for k in ks], first[0], False)); first[0] = False
-            tag[0] = "e%d%d" % (t, h)
-            eh, el = tile("bf", HQ), tile("bf", HQ)
-            tt(eh, ind(sl(H, 0, V), vnh), zh, ALU.max); tt(el, ind(sl(Lw, 0, V), vnh), zh, ALU.max)
-            mm(grp(G, [(Wb[t], eh), (nWb[t], el)], False, False))
-            ad = tile("bf", HQ); act(ad, d, ACT.Abs)
-            p = sl(ps(), 0, HQ); mm(grp(p, [(Bb, ad)]))
-            lk = tile("bf", HQ); ts(lk, p, TH + 0.5, ALU.is_lt)
-            mm(grp(G, [(nI4k, lk)], False, True))
-            p = sl(ps(), 0, HQ); mm(grp(p, [(I2, zh), (Ib, d)]))
-            r1 = tile("f32", HQ); hv = tile("bf", HQ); act(r1, p, None, MAGIC, 0.4995); act(hv, r1, None, -MAGIC)
-            p = sl(ps(), 0, HQ); mm(grp(p, [(Ih, mid), (Wt, hv)]))
-            r2 = tile("f32", HQ); qv = tile("bf", HQ); act(r2, p, None, MAGIC, 1.0 / V); act(qv, r2, None, -MAGIC)
-            p = ps(); pa, pb = sl(p, 0, HQ), sl(p, HQ, 2 * HQ)
-            mm(grp(pb, [(Ib, ad), (nIb, hv)]) + grp(pa, [(Bh, vw), (nWt, hv), (I2k, qv)]))
-            s2 = tile("hf", HQ); s3 = tile("bf", HQ); tt(s2, pa, lk, ALU.mult); tt(s3, pb, lk, ALU.mult)
-            p = ps(); pa, pb = sl(p, 0, HQ), sl(p, HQ, 2 * HQ)
-            mm(grp(pb, [(Ib, zh), (nIb, hv)]) + grp(pa, [(Wt, hv), (nI2k, qv), (Ih, s2)]))
-            zd = tile("bf", HQ); act(sl(M, V + q0, V + q0 + HQ), pa); act(zd, pb)
-            Lf = tile("hf", HQ); cp(Lf, Lh)
-            fa = tile("bf", HQ)
-            if cfg["faa"]: act(fa, G, ACT.Sign, -0.5 - TAU[t])
-            else: ts(fa, G, TAU[t] + 0.5, ALU.is_gt)
-            p = ps(); pa, pb = sl(p, 0, HQ), sl(p, HQ, 2 * HQ)
-            mm(grp(pb, [(Ih, Lf), (Wh[t], vw), (nIh, qr)])); mm(grp(pa, [(Tri, fa)]))
-            ov = tile("hf", 2 * HQ); oh, vc = sl(ov, 0, HQ), sl(ov, HQ, 2 * HQ)
-            ts(oh, pa, kf if cfg["faa"] else 0.5, ALU.is_gt); tt(vc, pb, oh, ALU.mult)
-            p = sl(ps(), 0, 14); nc = tile("f32", 8)
-            mm(grp(p, [(Ih, Qlist[h])], True, False) + relist(p, Wh, ov, 2 * HQ, False, True))
-            ts(sl(nc, 0, 7), sl(p, 0, 7), -float(V), ALU.mult, float(V), ALU.add); tt(sl(uf[h], 0, 7), sl(p, 7, 14), sl(nc, 0, 7), ALU.add)
-            uh = sl(ue, 8 * h, 8 * h + 7); cp(uh, sl(uf[h], 0, 7))
-            muh = sl(mu, q0, q0 + HQ); ts(muh, ind(sl(M, 0, V + q0 + HQ), uh), m012, ALU.mult)
-            if last:
-                p = sl(ps(), 0, 7)
-                mm(grp(p, [(W0[m], sl(muh, 7 * m, 7 * m + 7)) for m in range(16)])); act(sl(fin[h], 224, 231), p)
-            elif cfg["rl3"]:
-                for j in range(3): ts(sl(m3[h], 128 * j, 128 * j + HQ), muh, ke[j], ALU.mult)
-                p = sl(ps(), 0, 23); mm(relist(p, Wh, m3[h], 256 + HQ))
-                cp(sl(vl[t + 1], 8 * h, 8 * h + 7), sl(p, 0, 7)); cp(sl(nls[h], 0, 15), sl(p, 8, 23))
-            else:
-                p = sl(ps(), 0, 7); mm(relist(p, W0, muh, HQ)); cp(sl(vl[t + 1], 8 * h, 8 * h + 7), p)
-            p = ps(); pa, pb = sl(p, 0, HQ), sl(p, HQ, 2 * HQ)
-            mm(grp(pb, [(Bh, oh)])); s4 = tile("bf", HQ); tt(s4, pb, zd, ALU.mult)
-            mm(grp(pa, [(nIh, qr), (R0, muh)])); oa = tile("hf", HQ); tt(oa, pa, oh, ALU.mult)
-            p = sl(ps(), 0, HQ); mm(grp(p, [(Ib, hv), (Ib, s3), (Ib, s4)]))
-            act(sl(fin[h], HQ, 2 * HQ) if last else sl(z[t + 1], q0, q0 + HQ), p)
-            p = sl(ps(), 0, HQ); mm(grp(p, [(Ih, Lf), (Wh[t], vw), (nIh, vc), (Ih, oa)]))
-            if last:
-                act(sl(fin[h], 0, HQ), p)
-                send([(sl(fin[h], 0, 231), sl(finl[h], 0, 231))], 800)
-                cs = slice(q0, q0 + HQ)
-                dma("S", dram("yl", (A_, cs)), sl(finl[h], 0, HQ), 2200)
-                dma("S", dram("yz", (A_, cs)), sl(finl[h], HQ, 2 * HQ), 2200)
-                dma("S", dram("yv", (A_, cs)), sl(finl[h], 224, 231), 2200)
-            else:
-                ts(sl(Lo_[t + 1], q0, q0 + HQ), p, kn[t + 1], ALU.mult)
-                send([(sl(z[t + 1], q0, q0 + HQ), sl(zs[t + 1], q0, q0 + HQ)), (sl(Lo_[t + 1], q0, q0 + HQ), sl(Ls[t + 1], q0, q0 + HQ))], 500)
-            tag[0] = "u%d%d" % (t, h)
-            p = sl(ps(), 0, HQ); mm(grp(p, [(Ih, TriQ[h]), (nDB, oh), (Bh, vc)]))
-            act(sl(ubc, q0, q0 + HQ), p, None, float(V))
-        news = []
-        for h in range(2):
-            q0 = HQ * h; tag[0] = "u%d%d" % (t, h)
-            eq = tile("bf", HQ); tt(eq, ind(sl(uf[h], 0, 7), obc), sl(ubc, q0, q0 + HQ), ALU.is_equal)
-            dup = tile("bf", HQ); scan(dup, rzero, eq, ALU.mult, ALU.max)
-            o1 = tile("f32", 8); o2 = tile("f32", 8); so = tile("u16", 16)
-            if cfg["tia"]: act(sl(o1, 0, 7), sl(dup, 15, HQ, 16), None, 0.0, spare)
-            else: ts(sl(o1, 0, 7), sl(dup, 15, HQ, 16), spare, ALU.mult)
-            tt(sl(o2, 0, 7), sl(o1, 0, 7), sl(uf[h], 0, 7), ALU.max)
-            cp(sl(so, 0, 14, 2), sl(o2, 0, 7))
-            m32 = tile("f32", HQ); mn = tile("f32", HQ); hn, ln = tile("bf", HQ), tile("bf", HQ)
-            act(m32, ind(sl(M, 0, V + q0 + HQ), sl(ue, 8 * h, 8 * h + 7)))
-            p = sl(ps(), 0, HQ); mm(grp(p, [(Tm, m32)])); act(mn, p, None, ke[4])
-            if not last:
-                nl = nls[h]
-                if not cfg["rl3"]:
-                    for j in (1, 2): ts(sl(m3[h], 128 * j, 128 * j + HQ), sl(mu, q0, q0 + HQ), ke[j], ALU.mult)
-                    p = sl(ps(), 0, 15); mm(relist(p, Wh, sl(m3[h], 128, 384), 128 + HQ)); cp(sl(nl, 0, 15), p)
-                xa = tile("bf", HQ); act(xa, ind(X, sl(nl, 0, 7)))
-                tt(hn, ind(X, sl(nl, 8, 15)), xa, ALU.max); tt(ln, ind(X, sl(nl, 8, 15)), xa, ALU.min)
-            news.append((so, mn, hn, ln))
-        for h, (so, mn, hn, ln) in enumerate(news):
-            for tab, src, nm in ((M, mn, "m"),) if last else ((H, hn, "u"), (Lw, ln, "u"), (M, mn, "m")):
-                tag[0] = "%s%d%d" % (nm, t, h)
-                for b in range(7): cp(ind(tab, sl(so, 2 * b, 2 * b + 1)), sl(src, 16 * b, 16 * b + 16))
-    add("A", "dma", (dram("ya", (A_, A_)), ("rows", M, 6)), [sl(M, 0, V)], [], 60, 2400)
+                    end = lt and i == 1 and j == 3; ks = kk[4 * j:4 * j + 4]
+                    if sT: mm([(G, sl(cq, 0, n), Ib, True, False)] * (i + j == 0) +
+                              [(sl(G, k, 128, 16), sl(sg[i], 16 * q0 + k, 16 * q1, 16), (G8, nG8)[i], False, end and k == ks[-1]) for k in ks])
+                    else: mm(grp(G, [((Wb, nWb)[i][k], sl(sg[i], 16 * q0 + k, 16 * q1, 16)) for k in ks], i + j == 0, end))
+                    if fix and i == 1 and j == 0: mm(fix)
+            tag[0] = "f%d%d" % (t, h)
+            if not lt:
+                eh, el = tile("bf", n), tile("bf", n)
+                tt(eh, ind(H, vnh), zh, ALU.max); tt(el, ind(Lw, vnh), zh, ALU.max)
+                if sT: mm([(sl(G, t, 128, 16), eh, G8, False, False), (sl(G, t, 128, 16), el, nG8, False, True)])
+                else: mm(grp(G, [(Wb[t], eh), (nWb[t], el)], False, True))
+            if sT:
+                fT = sl(tile("bf", 128), 0, 128, 1, n); act(fT, G, ACT.Sign, -float(TAU[t]))
+                p = sl(ps(), 0, n); mm(grp(p, [(fT, sl(Ib, 0, n, 1, n))])); move(sl(fa, q0, q1), p)
+            else: act(sl(fa, q0, q1), G, ACT.Sign, -0.5 - TAU[t])
+        mu = tile("hf", Q); ul16 = tile("hf", 16); mn = tile("f32", Q); vcs = []; uB = []
+        for e, (q0, q1) in enumerate(esegs):
+            n = q1 - q0; b0, b1 = q0 // 16, q1 // 16; nb = b1 - b0; tag[0] = "e%d%d" % (t, e); sub = inside(q0, q1, segs)
+            zh = zland(t, q0, q1); xv = sl(xvl, q0, q1); lt = late[t][sub[0][0]]
 
-    n = len(ops); eng = [o["eng"] for o in ops]; cost = [o["cost"] for o in ops]; lat = [o["lat"] for o in ops]
-    tls = [o["tiles"] for o in ops]; hop, peek = cfg["hop"], cfg["peek"]
-    pred = [[(j, cost[j] + lat[j] + (cfg["same"] if eng[j] == eng[i] else hop) if hard else 0.0) for j, hard in ops[i]["deps"].items()] for i in range(n)]
-    succ = [[] for _ in range(n)]
+            def fresh(p, W):
+                return [] if lt else [(p, W, sl(vcl, q0, q1), False, False)]
+            ad, hv = sl(Zw[t][e], 0, n), sl(Zw[t][e], S, S + n)
+            p = sl(ps(), 0, n); mm(grp(p, [(nIb, zh), (Ib, xv)])); act(ad, p, ACT.Abs)
+            p = sl(ps(), 0, n); mm(grp(p, [(Ihalf, sl(cq, 0, n)), (Ihalf, zh), (Ihalf, xv)]))
+            if cfg["hva"]:
+                r1 = tile("f32", n); act(r1, p, None, MAGIC); act(hv, r1, None, -MAGIC)
+            else: ts(hv, p, MAGIC, ALU.add, MAGIC, ALU.subtract)
+            Lm = tile("hf", n); ts(Lm, sl(Ls[t], q0, q1), -F, ALU.add)
+            vn16 = tile("hf", nb); cp(vn16, sl(vnl, b0, b1))
+            ul, w, qq = [sl(tile(a, 128), 0, 128, 1, nb) for a in ("hf", "hf", "bf")]; Inb = sl(Ib, 0, nb, 1, nb)
+            p = sl(ps(), 0, 128, 1, nb); mm(blocks(p, ad, G8)); ts(ul, p, TH + 0.5, ALU.is_gt, float(S), ALU.mult)
+            p = sl(ps(), 0, 128, 1, nb); mm(blocks(p, hv, Wt8)); lin(qq, p, 4.0 * S, 159.5 + 0.5 / V)
+            p = sl(ps(), 0, 128, 1, nb)
+            mm([(p, sl(Icq[lt], 0, nb, 1, nb), sl(cq, 0, 128, 1, nb), True, False)] + blocks(p, hv, Wt8, False) +
+               (blocks(p, Lm, nR8[t], False) if lt else blocks(p, sl(vcl, q0, q1), nG8s, False)))
+            mm([(p, sl(nIq, 0, nb, 1, nb), qq, False, True)])
+            tt(w, p, ul, ALU.mult)
+            p = ps(); pa, pb = sl(p, 0, n), sl(p, 256, 256 + n)
+            mm(grp(pa, [(Bb, ad), (T8, sl(fa, q0, q1))]) + grp(pb, [(IrS, Lm)] + [x[1:3] for x in fresh(pb, Wr[t])]))
+            ov = tile("hf", 2 * n); oh, vc = sl(ov, 0, n), sl(ov, n, 2 * n); vcs.append(vc)
+            ts(oh, pa, thr, ALU.is_gt, float(S), ALU.mult); tt(vc, pb, oh, ALU.mult)
+            p = sl(ps(), 0, 2 * nb); pi_, pu = sl(p, 0, nb), sl(p, nb, 2 * nb)
+            lst = tolist(p, ov, Wb, G8, cfg["rl"][1]); uB.append(lst[0][1])
+            mm(lst + [(pi_, Ib, sl(Qlist, 0, nb), False, False), (pu, Ir8k, vn16, False, False), (pi_, ul, Inb, False, False), (pu, w, Inb, False, True)])
+            iu = tile("u16", 2 * nb); ts(iu, p, F, ALU.add); idx, ue = sl(iu, 0, nb), sl(iu, nb, 2 * nb)
+            if cfg["t1a"] and not last:
+                t1 = tile("f32", nb); act(t1, pu, ACT.Relu, 0.0, 8192.0)
+            else:
+                t1 = tile("hf", nb); ts(t1, pu, 8192.0, ALU.mult, 0.0, ALU.max)
+            m32 = tile("f32", n); move(m32, ind(Mw, ue))
+            muh = sl(mu, q0, q1); ts(muh, m32 if cfg["mum"] else ind(Mw, ue), m012, ALU.mult, -F, ALU.add)
+            zn = sl(fz if last else z[t + 1], q0, q1); move(zn, ind(sl(Zw[t][e], 0, 2 * S + n), idx))
+            if last:
+                send([(zn, sl(fzl, q0, q1))], 300)
+                dma("G", dram("yz", (A_, slice(q0, q1))), sl(fzl, q0, q1), 2600)
+                p = sl(ps(), 0, n)
+                mm([(p, Ihalf, sl(cq, 0, n), True, False)] + [(sl(p, m, n, 16), down[m], t1, False, False) for m in range(16)]); mm([(p, Ib, muh, False, True)])
+                lin(sl(fin[e], n, 2 * n), p, 1.0, F + 0.25)
+            else:
+                if not cfg["zl"]: send([(zn, zland(t + 1, q0, q1))], 300)
+                p = sl(ps(), 0, nb); mm(tolist(p, muh, W0, G80, cfg["rl"][2]) + [(p, I32 if cfg["t1a"] else Ib, t1, False, True)]); ts(sl(vl[t + 1], b0, b1), p, F, ALU.add)
+            p = sl(ps(), 0, n); mm(grp(p, [(R0r, muh)])); oa = tile("hf", n); tt(oa, p, oh, ALU.mult)
+            for h, a, b in sub: terms[h] = [(s, sl(x, a - q0, b - q0)) for s, x in ((1, Lm), (-1, vc), (1, oa))]
+            now = [(h, a, b) for h, a, b in sub if last or not late[t + 1][h] or not late[t][h]]
+            if now:
+                p = sl(ps(), 0, n); mm([(p, Ib, Lm, True, False)] + fresh(p, Wb[t]) + grp(p, [(nIb, vc), (Ib, oa)], False, True))
+            if last:
+                lin(sl(fin[e], 0, n), p, 1.0, F)
+                send([(fin[e], finl[e])], 800)
+                dma("S", dram("yl", (A_, slice(q0, q1))), sl(finl[e], 0, n), 2200)
+                dma("A", dram("yv", (A_, slice(q0, q1))), ("rows", sl(finl[e], n, 2 * n), 0, n), 2200, [sl(finl[e], n, 2 * n)])
+            else:
+                if len(now) == len(sub) and not any(late[t + 1][h] for h, a, b in now): now = [(now[0][0], q0, q1)]
+                for h, a, b in now:
+                    if late[t + 1][h]:
+                        Lx = tile("hf", b - a); cp(Lx, sl(p, a - q0, b - q0)); terms[h] = [(1, Lx)]
+                    else:
+                        ts(sl(Lo_[t + 1], a, b), sl(p, a - q0, b - q0), F, ALU.add, kn[t + 1], ALU.mult)
+                        send([(sl(Lo_[t + 1], a, b), sl(Ls[t + 1], a, b))] + [(zn, zland(t + 1, q0, q1))] * cfg["zl"], 300 + 200 * cfg["zl"])
+            tag[0] = "g%d%d" % (t, e)
+            if not byB: ts(sl(ul16, b0, b1), ue, -F, ALU.add)
+            p = sl(ps(), 0, n); mm(grp(p, [(Tm, m32)])); lin(sl(mn, q0, q1), p, 1.0, ke[4])
+        news = []
+        for u, (q0, q1) in enumerate(esegs if last and cfg["ulast"] else usegs):
+            n = q1 - q0; b0, b1 = q0 // 16, q1 // 16; nb = b1 - b0; tag[0] = "u%d%d" % (t, u)
+            p = sl(ps(), 0, n); uh = sl(ul16, b0, b1)
+            mm([(p, Ib, sl(TriD, 0, n), True, False)] +
+               [m for e, a, b in inside(q0, q1, esegs) for m in ((sl(p, a - q0, b - q0), nBr, vcs[e], False, False),
+                                                                 (sl(p, a - q0 + 15, b - q0, 16), Br, sl(vcs[e], 15, b - a, 16), False, False))])
+            parts = inside(q0, q1, esegs)
+            if byB: mm([(sl(p, a - q0, b - q0), uB[e], Rb[b - a], False, b == q1) for e, a, b in parts])
+            else: mm([(sl(p, m, n, 16), IrS, uh, False, m == 14) for m in range(15)])
+            prod = tile("bf", n); scan(prod, sl(rone, 0, n), p, ALU.add, ALU.mult)
+            tq = tile("hf", nb); ts(tq, sl(prod, 14, n, 16), 0.0, ALU.is_equal, 4096.0, ALU.mult)
+            p = sl(ps(), 0, nb)
+            if byB: mm([(p, Ib, tq, True, False)] + [(sl(p, (a - q0) // 16, (b - q0) // 16), uB[e], sl(Ib, (b - a) // 16, (b - a) // 8, 1, (b - a) // 8), False, b == q1) for e, a, b in parts])
+            else: mm(grp(p, [(Ib, uh), (Ib, tq)]))
+            so = tile("u16", 2 * nb); ts(sl(so, 0, 2 * nb, 2), p, spare, ALU.min, F, ALU.add)
+            news.append((so, q0, nb))
+            if not last:
+                s16 = tile("hf", nb); ts(s16, p, spare, ALU.min)
+                p = sl(ps(), 0, 2 * nb); mm([(sl(p, j, 2 * nb, 2), twice[j], s16, True, True) for j in range(2)])
+                so2 = tile("u16", 2 * nb); ts(so2, p, rTW, ALU.add)
+                p = sl(ps(), 0, 2 * nb); mm(grp(p, [(pair[s], sl(mu, q0 + s, q1, 8)) for s in range(8)]))
+                nl = tile("u16", 2 * nb); ts(nl, p, F, ALU.add)
+                xab, rr = tile("bf", 2 * n), tile("bf", 2 * n); move(xab, ind(X, nl))
+                p = sl(ps(), 0, n); mm(grp(p, [(nIb, sl(xab, 0, 2 * n, 2)), (Ib, sl(xab, 1, 2 * n, 2))]))
+                relu(sl(rr, 0, 2 * n, 2), p); lin(sl(rr, 1, 2 * n, 2), sl(rr, 0, 2 * n, 2), -1.0, 0.0, "V")
+                news[-1] += (so2, xab, rr)
+        for h, nw in enumerate(news):
+            so, q0, nb = nw[:3]; tag[0] = "m%d%d" % (t, h)
+            for b in range(nb): cp(ind(M, sl(so, 2 * b, 2 * b + 1)), sl(mn, q0 + 16 * b, q0 + 16 * b + 16))
+            if not last:
+                so2, xab, rr = nw[3:]; tag[0] = "h%d%d" % (t, h)
+                for b in range(nb): tt(ind(HL, sl(so2, 2 * b, 2 * b + 2)), sl(xab, 32 * b, 32 * b + 32), sl(rr, 32 * b, 32 * b + 32), ALU.add)
+    dma("S", dram("ya", (A_, A_)), ("rows", M, 6, V), 2400, [sl(M, 0, V)])
+
+    n = len(ops); tls = [o["tiles"] for o in ops]; peek = cfg["peek"]; cases = cfg["cases"]; hop = cases[0][7]
+    reach = []; dep = []
     for i in range(n):
-        for j, w in pred[i]: succ[j].append((i, w))
-    back = [[(i, max(0.0, w - cost[j]) + cost[i] if w else 0.0) for i, w in succ[j]] for j in range(n)]
-    bsucc = [[] for _ in range(n)]
-    for j in range(n):
-        for i, w in back[j]: bsucc[i].append((j, w))
+        hard = [j for j, h in ops[i]["deps"].items() if h]; below = 0
+        for j in hard: below |= reach[j]
+        dep.append([(j, h) for j, h in ops[i]["deps"].items() if not below >> j & 1])
+        for j in hard: below |= 1 << j
+        reach.append(below)
+    eng, cost, lat = [None] * n, [0.0] * n, [0.0] * n
+    costs = [[0.0] * n for _ in cases]; lats = [[o["lat"][0] * c[5] + o["lat"][1] * c[6] for o in ops] for c in cases]
+    pred, succ, back, bsucc = [], [], [], []
+
+    def choose(pick):
+        for i, o in enumerate(ops):
+            a = o["alts"][pick[i]]; eng[i] = a[0]
+            for c, cs in zip(cases, costs): cs[i] = sum(x * y for x, y in zip(a[3], c))
+        cost[:] = costs[0]; lat[:] = lats[0]; same = cases[0][8]
+        pred[:] = [[(j, cost[j] + lat[j] + (same if eng[j] == eng[i] else hop) if h else 0.0) for j, h in dep[i]] for i in range(n)]
+        succ[:] = [[] for _ in range(n)]; bsucc[:] = [[] for _ in range(n)]
+        for i in range(n):
+            for j, w in pred[i]: succ[j].append((i, w))
+        back[:] = [[(i, max(0.0, w - cost[j]) + cost[i] if w else 0.0) for i, w in succ[j]] for j in range(n)]
+        for j in range(n):
+            for i, w in back[j]: bsucc[i].append((j, w))
+
+    def judge(f):
+        if not f: return None
+        more = {}; out = []
+        for i, j in f[4]: more.setdefault(i, []).append((j, eng[j] != eng[i]))
+        for c, cs, ls in zip(cases, costs, lats):
+            st = [0.0] * n; free = {e: 0.0 for e in "VAPGS"}; end = 0.0; hp, sm = c[7], c[8]
+            for i in f[2]:
+                e = eng[i]; s = free[e]
+                for j, h in dep[i] + more[i] if i in more else dep[i]:
+                    if h:
+                        x = st[j] + cs[j] + ls[j] + (sm if eng[j] == e else hp)
+                        if x > s: s = x
+                st[i] = s; free[e] = s + cs[i]
+                if s + cs[i] + ls[i] > end: end = s + cs[i] + ls[i]
+            out.append(end)
+        return (sum(x / c[9] for x, c in zip(out, cases)) / len(cases) * cases[0][9] + fullest(),) + f[1:] + (out,)
+
+    def fullest():
+        return cfg["even"] * max(sum(c for c, e in zip(costs[0], eng) if e == x) for x in "VA")
     uses = {tl: len(set(a[0] for a in lst)) for tl, lst in psacc.items()}
 
-    def run(pr, pre_, suc_, av0):
-        left = dict(uses); bank, held, lastuse, bfree, extra = {}, [None] * 8, [[] for _ in range(8)], [0.0] * 8, []
+    def run(pr, pre_, suc_, av0, banks=8):
+        left = dict(uses); bank, held, lastuse, bfree, extra = {}, [None] * banks, [[] for _ in range(banks)], [0.0] * banks, []
         miss = [len(x) for x in pre_]; st = [0.0] * n; av = list(av0); free = {e: 0.0 for e in "VAPGS"}; order = []
-        ready = [i for i in range(n) if miss[i] == 0]
-        while ready:
-            fb = [x for x in range(8) if held[x] is None]; b0 = min(fb, key=lambda x: bfree[x]) if fb else None
-            cand = []; s0 = 1e18; e0 = None
-            for i in ready:
-                s = max(av[i], free[eng[i]]); new = bool(tls[i]) and any(tl not in bank for tl in tls[i])
-                if new:
-                    if b0 is None: continue
-                    s = max(s, bfree[b0])
-                cand.append((s, i, new))
-                if s < s0: s0, e0 = s, eng[i]
-            if not cand: return None
-            s, i, new = max([c for c in cand if eng[c[1]] == e0 and c[0] <= s0 + peek], key=lambda c: pr[c[1]])
-            if new:
-                tl = [x for x in tls[i] if x not in bank][0]; bank[tl] = b0; held[b0] = tl
-                extra += [(i, j) for j in lastuse[b0]]; lastuse[b0] = []
-            for tl in tls[i]:
+        ready = {e: [i for i in range(n) if miss[i] == 0 and eng[i] == e] for e in "VAPGS"}
+        for step in range(n):
+            fb = [x for x in range(banks) if held[x] is None]; b0 = min(fb, key=lambda x: bfree[x]) if fb else None
+            s0 = 1e18; e0 = None; bf = bfree[b0] if fb else 1e18
+            for e, lst in ready.items():
+                for i in lst:
+                    s = av[i]
+                    if tls[i] and tls[i][0] not in bank and bf > s: s = bf
+                    if free[e] > s: s = free[e]
+                    if s < s0: s0, e0 = s, e
+            if s0 >= 1e18: return None
+            i = -1; lim = s0 + peek
+            for k in ready[e0]:
+                if av[k] <= lim and (i < 0 or pr[k] > pr[i]) and not (tls[k] and tls[k][0] not in bank and bf > lim): i = k
+            s = max(av[i], free[e0])
+            if tls[i]:
+                tl = tls[i][0]
+                if tl not in bank:
+                    s = max(s, bf); bank[tl] = b0; held[b0] = tl
+                    extra += [(i, j) for j in lastuse[b0]]; lastuse[b0] = []
                 b = bank[tl]; lastuse[b].append(i); left[tl] -= 1; bfree[b] = max(bfree[b], s + cost[i] + lat[i] + hop)
                 if left[tl] == 0: held[b] = None
-            st[i] = s; free[eng[i]] = s + cost[i]; order.append(i); ready.remove(i)
+            st[i] = s; free[e0] = s + cost[i]; order.append(i); ready[e0].remove(i)
             for j, w in suc_[i]:
                 if s + w > av[j]: av[j] = s + w
                 miss[j] -= 1
-                if miss[j] == 0: ready.append(j)
+                if miss[j] == 0: ready[eng[j]].append(j)
         return max(st[i] + cost[i] + lat[i] for i in range(n)), st, order, bank, extra
-    pr = [0.0] * n
-    for i in range(n - 1, -1, -1): pr[i] = max([pr[j] + w for j, w in succ[i]] + [cost[i] + lat[i]])
-    pr = [x + cfg["bias"].get(o["tag"], 0.0) for x, o in zip(pr, ops)]
-    best = run(pr, pred, succ, [0.0] * n); cur = best; rnd = [cfg["seed"]]
-    tags = sorted(set(o["tag"] + o["eng"] for o in ops))
+    zero = [0.0] * n; rnd = [cfg["seed"]]
+    kind_ = [o["tag"] + o["eng"] for o in ops]; tags = sorted(set(kind_))
+    free_ = [i for i, o in enumerate(ops) if len(o["alts"]) > 1]; pick = [0] * n; choose(pick)
 
     def draw():
         rnd[0] = (rnd[0] * 6364136223846793005 + 1442695040888963407) % 2 ** 64
         return (rnd[0] >> 33) / 2.0 ** 31
+    pr = [0.0] * n; after = {}
+    for i in range(n - 1, -1, -1):
+        pr[i] = max([pr[j] + w for j, w in succ[i]] + [cost[i] + lat[i]] + ([pr[after[kind_[i]]] + cost[i]] if kind_[i] in after else []))
+        after[kind_[i]] = i
+    best = cur = judge(run(pr, pred, succ, zero)); curp = pr; bestpick = pick; now = pick
     for it in range(cfg["rounds"]):
-        amp = 3000.0 * draw() ** 2; nz = {tg: amp * (draw() - 0.5) for tg in tags}
-        r = run([cur[1][i] + cost[i] + nz[ops[i]["tag"] + eng[i]] for i in range(n)], back, bsucc, lat) if cur else None
-        f = run([r[1][i] + cost[i] for i in range(n)], pred, succ, [0.0] * n) if r else None
-        if f and (best is None or f[0] < best[0]): best = f
-        cur = f if f and f[0] < best[0] * 1.02 else best
-    _, st_t, order, bank, extra = best
+        p3 = pick
+        if draw() < cfg["pflip"]:
+            p3 = list(pick)
+            for _ in range(1 + int(2 * draw())):
+                i = free_[int(len(free_) * draw())]; p3[i] = (p3[i] + 1) % len(ops[i]["alts"])
+        if p3 is not now: choose(p3); now = p3
+        if p3 is not pick and cur and draw() < 0.6: p2 = [-x for x in cur[1]]
+        elif cur and draw() < cfg["pback"]:
+            amp = 2000.0 * draw() ** 2; nz = {tg: amp * (draw() - 0.5) for tg in tags}
+            r = run([cur[1][i] + cost[i] + nz[kind_[i]] for i in range(n)], back, bsucc, lat, cfg["bb"])
+            p2 = [r[1][i] + cost[i] for i in range(n)] if r else None
+        else:
+            base = [-x for x in cur[1]] if cur and draw() < 0.5 else curp
+            nz = {tg: 0.0 for tg in tags}
+            for _ in range(1 + int(3 * draw())): nz[tags[int(len(tags) * draw())]] = 6000.0 * draw() ** 2 * (1 if draw() < 0.5 else -1)
+            p2 = [base[i] + nz[kind_[i]] for i in range(n)]
+        f = judge(run(p2, pred, succ, zero)) if p2 else None
+        if f and (best is None or f[0] < best[0]): best, bestpick = f, p3
+        if f and (cur is None or f[0] < cur[0] + cfg["temp"] * (1.0 - it / cfg["rounds"]) * draw()): cur, curp, pick = f, p2, p3
+    _, st_t, order, bank, extra, ends = best; choose(bestpick)
+    alld = [list(d) for d in dep]
+    for i, j in extra: alld[i].append((j, 2))
+    outs = [[] for _ in range(n)]
+    for i in range(n):
+        for j, h in alld[i]: outs[j].append(i)
+
+    def replay(seq):
+        miss = [len(d) for d in alld]; at = {e: 0 for e in seq}; od = []; go_ = True
+        while go_:
+            go_ = False
+            for e, q in seq.items():
+                k = at[e]
+                while k < len(q) and miss[q[k]] == 0:
+                    od.append(q[k])
+                    for j in outs[q[k]]: miss[j] -= 1
+                    k += 1
+                if k > at[e]: at[e] = k; go_ = True
+        if len(od) < n: return None
+        res = []
+        for c, cs, ls in zip(cases, costs, lats):
+            st = [0.0] * n; why = [-1] * n; free = {e: (0.0, -1) for e in seq}; end = 0.0; hp, sm = c[7], c[8]; top_ = 0
+            for i in od:
+                e = eng[i]; s, y = free[e]
+                for j, h in alld[i]:
+                    if h == 1 or (h and eng[j] != e):
+                        x = st[j] + cs[j] + ls[j] + (sm if eng[j] == e else hp)
+                        if x > s: s, y = x, j
+                st[i] = s; why[i] = y; s += cs[i]; free[e] = (s, i)
+                if s + ls[i] > end: end, top_ = s + ls[i], i
+            res.append((end, st, why, top_))
+        return sum(r[0] / c[9] for r, c in zip(res, cases)) / len(cases) * cases[0][9] + fullest(), od, res
+
+    def seteng(i, k):
+        a = ops[i]["alts"][k]; eng[i] = a[0]
+        for c, cs in zip(cases, costs): cs[i] = sum(x * y for x, y in zip(a[3], c))
+    seq = {e: [i for i in order if eng[i] == e] for e in "VAPGS"}; pick = list(bestpick)
+    cur = replay(seq); best = (cur, dict(seq), list(pick))
+    for it in range(cfg["polish"]):
+        end, st, why, i = cur[2][int(len(cases) * draw())]; path = []
+        while i >= 0: path.append(i); i = why[i]
+        i = path[int(len(path) * draw())]; e = eng[i]; q = seq[e]; k = q.index(i); new = dict(seq); u = draw(); old = pick[i]
+        if len(ops[i]["alts"]) > 1 and u < 0.3:
+            pick[i] = (old + 1) % len(ops[i]["alts"]); seteng(i, pick[i]); new[e] = q[:k] + q[k + 1:]; q2 = seq[eng[i]]
+            k2 = max(0, sum(1 for j in q2 if st[j] < st[i]) - int(2 * draw())); new[eng[i]] = q2[:k2] + [i] + q2[k2:]
+        elif u < 0.7:
+            d = 1 + int(4 * draw() ** 2); k2 = max(0, k - d); new[e] = q[:k2] + [i] + q[k2:k] + q[k + 1:]
+        else:
+            d = 1 + int(4 * draw() ** 2); new[e] = q[:k] + q[k + 1:k + 1 + d] + [i] + q[k + 1 + d:]
+        f = replay(new)
+        if f and f[0] < cur[0] + cfg["temp2"] * (1.0 - it / cfg["polish"]) * draw():
+            cur, seq = f, new
+            if f[0] < best[0][0]: best = (f, dict(new), list(pick))
+        elif pick[i] != old: pick[i] = old; seteng(i, old)
+    bestpick = best[2]; choose(bestpick); order = best[0][1]; st_t = best[0][2][0][1]; ends = [r[0] for r in best[0][2]]; best = best[0]
+    order = sorted(order, key=lambda i, pos={j: k for k, j in enumerate(order)}: (st_t[i], pos[i]))
+    for i, o in enumerate(ops): o["eng"], o["kind"], o["args"] = o["alts"][bestpick[i]][:3]; o["cost"] = cost[i]
     fin_t = [st_t[i] + cost[i] + lat[i] for i in range(n)]
     for i, j in extra: ops[i]["deps"][j] = ops[i]["deps"].get(j, False) or eng[j] != eng[i]
 
@@ -480,7 +674,7 @@ def plan(cfg):
             clock[i] = {} if o["kind"] == "send" else dict(kn_)
             clock[i][sig[i][0]] = sig[i][1]
         prog.append((o, [(sig[j], ops[j]) for j in waits], sig.get(i)))
-    return {"prog": prog, "bank": bank, "top": top, "cnt": cnt, "nd": nd[0], "end": max(fin_t), "ops": ops, "st": st_t, "fin": fin_t, "order": order, "pr": pr}
+    return {"prog": prog, "bank": bank, "top": top, "cnt": cnt, "nd": nd[0], "end": max(fin_t), "ops": ops, "st": st_t, "fin": fin_t, "order": order, "ends": ends, "score": best[0]}
 
 
 PLAN = plan(CFG)
@@ -506,7 +700,7 @@ def rank_program(g, core, T, topo):
         if not isinstance(r, tuple): return r
         if r[0] == "ind": return ap(r[1]).indirect(ap(r[2]))
         if r[0] == "dram": return T[r[1]][r[2]]
-        if r[0] == "rows": return T["s_" + r[1][0]][r[2]:128:16, r[1][1]:r[1][1] + V]
+        if r[0] == "rows": return T["s_" + r[1][0]][r[2]:128:16, r[1][1]:r[1][1] + r[3]]
         buf = T["ps%d" % PLAN["bank"][r[5]]] if r[0] == "ps" else T["s_" + r[0]]
         return buf[0:r[4], r[1]:r[2]] if r[3] == 1 else buf[0:r[4], r[1]:r[2]:r[3]]
 

from concourse.bass import DstId, RemoteDMATransfer
from concourse.mybir import AluOpType, ActivationFunctionType

ALU = AluOpType
ACT = ActivationFunctionType
V, Q, NV = 2048, 224, 3
TH, TAU = 1020, (1020, 1530, 1275)
MAGIC = 12582912.0
BIG = 4194304.0
TW = V + 32
CQ = 32

CFG = {
    "segs": [(0, 128), (128, 224)], "esegs": [(0, 128), (128, 224)], "usegs": [(0, 128), (128, 224)],
    "late": ["00", "00", "00"],
    "wmode": ["aaaaaaa", "aaaaaaa", "aaaaaaa"],
    "hmode": ["vvavvav", "vvavvav", "vvavvav"],
    "lmode": ["vvavvav", "vvavvav", "vvavvav"],
    "zg": [[12, 12], [12, 12], [12, 12]], "t1a": False, "ulast": True,
    "sT": True, "rl": "pvp", "ne": 2, "xat": 1, "nr": 2,
    "zl": False, "mum": False, "hva": False,
    "seed": 2, "rounds": 600, "temp": 800.0, "pback": 0.4, "pflip": 0.25, "polish": 11000, "temp2": 150.0, "even": 0.1, "bb": 12, "peek": 30.0,
    "cases": [(1.0, 1.6, 3.9, 0.55, 300.0, 1.0, 2600.0, 110.0, 70.0, 90000.0),
              (0.9, 1.25, 2.8, 0.48, 500.0, 1.0, 3300.0, 110.0, 70.0, 86000.0),
              (1.2, 2.2, 5.5, 0.65, 300.0, 1.1, 2600.0, 130.0, 80.0, 112000.0)],
}
DT = {"bf": "bfloat16", "hf": "float16", "f32": "float32", "i32": "int32", "u16": "uint16"}


def plan(cfg):
    ops, top, acc, psacc = [], {a: 0 for a in DT}, {a: [] for a in DT}, {}
    nps = [0]; tag = ["i"]; dry = []
    w2 = {"bf": True, "hf": True, "f32": False, "i32": False, "u16": True, "ps": False}

    def tile(a, n):
        lo = (top[a] + 15) // 16 * 16
        top[a] = lo + n
        return (a, lo, lo + n, 1, 128, None)

    def ps():
        nps[0] += 1
        return ("ps", 0, 512, 1, 128, nps[0] - 1)

    def sl(r, a, b, step=1, p=None):
        return (r[0], r[1] + a, r[1] + b, step, r[4] if p is None else p, r[5])

    def wd(r):
        if r[0] == "ind": return 16 * wd(r[2])
        return (r[2] - r[1] + r[3] - 1) // r[3]

    def ind(win, off):
        return ("ind", win, off)

    def isref(x):
        return isinstance(x, tuple)

    def either(*ways):
        dry.append([])
        for f in ways: f()
        got = dry.pop()
        add(got[0][0], got[0][1], got[0][2], [r for x in got for r in x[4]], got[0][5], got[0][3], alts=[x[:4] for x in got])

    def add(eng, kind, args, rd, wr, cost, lat=(0.0, 0.0), alts=None):
        if dry: return dry[-1].append((eng, kind, args, cost, rd, wr))
        me = len(ops); deps = {}
        rr, ww = [], []
        for r in rd:
            if r[0] == "ind": rr += [r[1], r[2]]
            else: rr.append(r)
        for r in wr:
            if r[0] == "ind": ww.append(r[1]); rr.append(r[2])
            else: ww.append(r)
        dma = kind in ("dma", "send")
        tiles = []
        for isw, lst in ((False, rr), (True, ww)):
            for r in lst:
                if r[0] == "dram": continue
                if r[0] == "ps":
                    tiles.append(r[5])
                    for o, ow, lo, hi in psacc.setdefault(r[5], []):
                        if o == me: continue
                        hard = ops[o]["eng"] != eng or alts is not None or len(ops[o]["alts"]) > 1 or (ow and not isw and lo < r[2] and r[1] < hi)
                        deps[o] = deps.get(o, False) or hard
                    psacc[r[5]].append((me, isw, r[1], r[2]))
                    continue
                keep = []
                for e in acc[r[0]]:
                    o, ow, lo, hi, st = e
                    if o != me and (ow or isw) and lo < r[2] and r[1] < hi and not (st == r[3] > 1 and (lo - r[1]) % st):
                        deps[o] = True
                        if isw and r[3] == 1 and r[4] == 128 and r[1] <= lo and hi <= r[2]: continue
                    keep.append(e)
                acc[r[0]] = keep + [(me, isw, r[1], r[2], r[3])]
        ops.append({"eng": eng, "deps": deps, "lat": lat, "dma": dma, "alts": alts or [(eng, kind, args, cost)],
                    "tiles": sorted(set(tiles)), "tag": tag[0]})

    def vcost(out, ins, per):
        if out[0] == "ind": return (50, 0, wd(out))
        if ins[0][0] == "ind": return (50, wd(out))
        return (max(64.0, per * wd(ins[0])) + 10,)

    def cp(out, i):
        add("V", "cp", (out, i), [i], [out], vcost(out, [i], 0.5 if i[0] != "ind" and out[0] != "ind" and w2[i[0]] and w2[out[0]] else 1))

    def tt(out, a, b, op):
        add("V", "tt", (out, a, b, op), [a, b], [out], vcost(out, [a, b], 1 if "ps" in (a[0], b[0]) else 2))

    def ts(out, a, s1, op0, s2=None, op1=None):
        add("V", "ts", (out, a, s1, s2, op0, op1), [a] + [s for s in (s1, s2) if isref(s)], [out],
            vcost(out, [a], 0.5 if a[0] != "ind" and w2[a[0]] and w2[out[0]] else 1))

    def scan(out, d0, d1, op0, op1):
        add("V", "scan", (out, d0, d1, op0, op1), [d0, d1], [out], vcost(out, [d0], 0.5 if w2[d0[0]] and w2[d1[0]] and w2[out[0]] else 1))

    def mset(out, c):
        add("V", "mset", (out, c), [], [out], (max(64, wd(out)),))

    def act(out, i, f=None, bias=0.0, scale=1.0):
        add("A", "act", (out, i, f or ACT.Identity, bias, scale), [i] + [s for s in (bias, scale) if isref(s)], [out],
            (65, wd(out)) if i[0] == "ind" else (max(64, wd(out)) + 30,))

    def mm(lst):
        c = sum(max(min(64, wd(m[1])), wd(m[2])) * (1 if w2[m[2][0]] else 4) for m in lst)
        add("P", "mm", lst, [m[1] for m in lst] + [m[2] for m in lst], [m[0] for m in lst], (4 * len(lst), 0, 0, c), (60.0, 0.0))

    def move(out, i, first="A"):
        either(*[lambda: act(out, i), lambda: cp(out, i)][::1 if first in "Aa" else -1])

    def lin(out, i, scale, bias, first="A"):
        either(*[lambda: act(out, i, None, bias, scale), lambda: ts(out, i, scale, ALU.mult, bias, ALU.add)][::1 if first == "A" else -1])

    def relu(out, i):
        either(lambda: act(out, i, ACT.Relu), lambda: ts(out, i, 0.0, ALU.max))

    def grp(out, pairs, start=True, stop=True):
        return [(out, a, b, start and j == 0, stop and j == len(pairs) - 1) for j, (a, b) in enumerate(pairs)]

    def relist(out, W, src, start=True, stop=True):
        return grp(out, [(W[m], sl(src, m, wd(src), 16)) for m in range(16)], start, stop)

    def iota(out, pat, base=0, cm=0):
        add("G", "iota", (out, pat, base, cm), [], [out], (130 + 2 * wd(out),))

    def asel(out, i, pat, op, fill, base, cm):
        add("G", "asel", (out, i, pat, op, fill, base, cm), [i], [out], (170 + 2 * wd(out),))

    def spread(dst, src, on_g):
        n = wd(src)
        for k in range(16):
            o = sl(dst, k, 16 * n, 16)
            either(*[lambda: asel(o, src, [[0, n]], ALU.is_gt, 0.0, 1, 0), lambda: cp(o, src)][::1 if k < on_g else -1])

    def dma(eng, out, i, lat, rd=None):
        add(eng, "dma", (out, i), rd or [i], [out], (60,), (lat, 0.0))

    def send(pairs, by):
        add("G", "send", pairs, [p[0] for p in pairs], [p[1] for p in pairs], (0, 0, 0, 0, 1), (0.0, 1.0 + by / 2600.0))

    def dram(name, idx):
        return ("dram", name, idx)

    A_ = slice(None); segs, esegs, usegs = cfg["segs"], cfg["esegs"], cfg["usegs"]; F = float(V)
    late = [[c == "1" for c in s] for s in cfg["late"]]
    S = 128 if max(b - a for a, b in esegs) <= 128 else 256

    def inside(a, b, parts):
        return [(h, x, y) for h, (x, y) in enumerate(parts) if a <= x and y <= b]
    E = tile("i32", V); X = tile("bf", V); v0 = tile("i32", 16); L0 = tile("i32", Q)
    z = [tile("bf", Q) for _ in range(NV)]
    dma("A", sl(v0, 0, 14), dram("v0", (A_, A_)), 2000)
    ne = cfg["ne"]; ce = V // ne; at = 2000
    for j in range(ne + 1):
        if j == cfg["xat"]:
            at += 1700; dma("S", X, dram("X", (A_, A_)), at)
        if j < ne:
            at += 3400 // ne; dma("S", sl(E, ce * j, ce * j + ce), dram("E", (A_, slice(ce * j, ce * j + ce))), at)
    dma("A", z[0], dram("z0", (A_, A_)), 2300)
    dma("A", L0, dram("L0", (A_, A_)), 2600)

    pi = tile("i32", 16); iota(sl(pi, 0, 1), [[0, 1]], 0, 1)
    col = tile("f32", 160); iota(col, [[1, 160]])
    colk = tile("f32", 128); iota(colk, [[0, 8], [1, 16]])
    colg = tile("f32", 128); iota(colg, [[16, 8], [0, 16]])
    oi = tile("i32", 16); iota(sl(oi, 0, 8), [[1, 8]])
    olast = sl(tile("u16", 16), 0, 8); cp(olast, sl(oi, 0, 8))
    C = tile("f32", 32)
    cc = [sl(C, j, j + 1) for j in range(32)]
    ki = tile("i32", 16); ts(sl(ki, 0, 1), sl(pi, 0, 1), 15, ALU.bitwise_and); ts(sl(ki, 1, 2), sl(pi, 0, 1), 1, ALU.bitwise_and)
    pf, kf, gb = cc[0], cc[1], cc[2]
    cp(pf, sl(pi, 0, 1)); cp(kf, sl(ki, 0, 1)); tt(gb, pf, kf, ALU.subtract)
    KE = tile("f32", 16); ts(KE, sl(col, 0, 16), kf, ALU.is_equal)
    KN = tile("f32", 16); ts(KN, sl(col, 0, 16), kf, ALU.not_equal)
    ke = [sl(KE, j, j + 1) for j in range(16)]; kn = [sl(KN, j, j + 1) for j in range(16)]

    def times(src, s, a="bf"):
        t = tile(a, wd(src)); lin(t, src, s, 0.0); return t

    def timev(src, s, s2=None):
        if s2 is None: return times(src, s)
        t = tile("bf", wd(src)); ts(t, src, s, ALU.mult, s2, ALU.mult); return t

    def cuts(t):
        return [sl(t, 15 - m, 143 - m) for m in range(16)]

    def summed(a, parts):
        p = sl(ps(), 0, 128); mm(grp(p, [(Ib, x) for x in parts])); t = tile(a, 128); act(t, p); return t
    p16, g15 = cc[20], cc[3]; ts(p16, pf, 16.0, ALU.add); ts(g15, gb, 15.0, ALU.add)
    Iw = tile("bf", 160); ts(Iw, col, p16, ALU.is_equal)
    down = [sl(Iw, 16 + m, 144 + m) for m in range(16)]
    Ib = down[0]; J = down[4]
    nIb, Ihalf, IrS, Ir8k = [timev(Ib, s) for s in (-1.0, 0.5, 1.0 / S, 1 / 8192.0)]
    if cfg["t1a"] or "a" in cfg["rl"]: I32 = times(Ib, 1.0, "f32")
    Ww = tile("bf", 144); ts(Ww, sl(col, 0, 144), g15, ALU.is_equal)
    wt, k1 = cc[4], cc[6]
    ts(wt, kf, 2.0, ALU.mult, 1.0, ALU.add); ts(k1, kf, 1.0, ALU.add)
    Wb = cuts(Ww); W0, W1 = [cuts(times(Ww, s)) for s in (ke[0], ke[1])]
    Bb = tile("bf", 128); ts(Bb, colg, gb, ALU.is_equal)
    nBr, R0r, Br = times(Bb, -1.0 / S), timev(Bb, ke[0], 1.0 / S), times(Bb, 1.0 / S)
    G8 = sl(Bb, 0, 128, 16); G32 = times(G8, 32.0)
    anyl = any(any(x) for x in late)
    sg_ = 1.0 / (8192 * S); Wt8, nG8s = timev(G8, wt, sg_), times(G8, -sg_); I16 = sl(Ib, 0, 16)
    G80 = times(G8, ke[0]) if cfg["rl"][2] != "p" else None
    nIq = timev(I16, -F * sg_); Icq = [timev(I16, -2.0 * c * F * sg_) for c in (160, 159)[:1 + anyl]]
    nR8 = [timev(G8, ke[t], -sg_) if any(late[t]) else None for t in range(NV)]

    def blocks(out, src, G, one=True):
        return [(sl(out, m, 128, 16), sl(src, m, wd(src), 16), G, one, one) for m in range(16)]

    def tolist(out, src, W, G, how, stop=False):
        if how == "p": return relist(out, W, src, True, stop)
        k = wd(out); p = sl(ps(), 0, 128, 1, k); mm(blocks(p, src, G))
        u = sl(tile("f32" if how == "a" else "hf", 128), 0, 128, 1, k); (move if how == "a" else cp)(u, p)
        return [(out, u, sl(I32 if how == "a" else Ib, 0, k, 1, k), True, stop)]
    if cfg["sT"]: nG8 = times(G8, -1.0)
    else: nWb = cuts(times(Ww, -1.0)); nBb = times(Bb, -1.0)
    Kc = tile("bf", 128); act(Kc, colk, None, kf, 0.0)
    nK0 = timev(Ib, ke[0], -2.0); cq = tile("bf", Q); mset(cq, -0.5)
    rbig = tile("f32", 128); ts(rbig, colk, 0.0, ALU.is_equal, BIG, ALU.mult)
    nu = max(b - a for a, b in usegs); rone = tile("bf", nu); TriD = tile("bf", nu); tri = tile("bf", 128)
    ts(tri, colk, kf, ALU.is_ge, 4096.0 / S, ALU.mult)
    for a in range(0, nu, 128):
        b = min(nu, a + 128)
        ts(sl(rone, a, b), sl(colk, 0, b - a), 0.0, ALU.is_equal)
        asel(sl(TriD, a, b), sl(tri, 0, b - a), [[0, (b - a) // 16], [-1, 16]], ALU.not_equal, 0.0, 15, 0)
    byB = cfg["rl"][1] == "v"; Rb = {}
    for n in sorted(set(b - a for a, b in esegs)) if byB else []:
        r0 = tile("bf", n); r1 = tile("f32", n); iota(r1, [[1, n // 16], [0, 16]], n // 16, -1)
        ts(r0, r1, 0.0, ALU.is_equal, 1.0 / S, ALU.mult); Rb[n] = sl(tile("bf", n), 0, n, 1, n // 8)
        asel(sl(Rb[n], 0, n, 1, 128), r0, [[0, n // 16], [-1, 16]], ALU.not_equal, 0.0, 15, 0)
    T8 = tile("bf", 128); tmpa = tile("bf", 128)
    asel(tmpa, times(Bb, -8192.0), [[1, 128]], ALU.is_gt, 0.0, 0, -1); asel(T8, tmpa, [[1, 128]], ALU.not_equal, 8192.0, 0, -1)
    thr, qb = cc[21], cc[22]; ts(thr, kf, 8192.0, ALU.mult, 8192.0 + TH + 0.5, ALU.add); ts(qb, kf, -F, ALU.add)
    Qlist = sl(tile("hf", 16), 0, 14); ts(Qlist, sl(col, 0, 14), 16.0, ALU.mult, qb, ALU.add)
    m012, m16, spare, m03, m12, rTW = cc[7], cc[8], cc[10], cc[11], cc[23], cc[24]
    ts(m012, kf, 2.5, ALU.is_lt); ts(m03, kf, 3.5, ALU.is_lt); tt(m12, m012, ke[0], ALU.subtract)
    tt(cc[12], ke[4], ke[5], ALU.add); ts(m16, cc[12], 16.0, ALU.mult); ts(spare, kf, 1.0, ALU.add)
    ts(rTW, sl(ki, 1, 2), float(TW), ALU.mult, F, ALU.add)
    Vw = times(Iw, m12); pair = [sl(Vw, 17 - 2 * s, 145 - 2 * s) for s in range(8)]
    colh = tile("f32", 128); iota(colh, [[16, 8], [1, 8], [0, 2]])
    twice = [tile("bf", 128) for _ in range(2)]; ts(cc[25], pf, -8.0, ALU.add)
    ts(twice[0], colh, pf, ALU.is_equal); ts(twice[1], colh, cc[25], ALU.is_equal)
    Mi = summed("bf", [times(Ib, m03), times(Wb[6], k1), Wb[7]])
    tt(cc[17], m03, ke[0], ALU.subtract); ts(cc[18], ke[0], 16.0, ALU.mult, ke[6], ALU.add); tt(cc[19], cc[18], ke[7], ALU.subtract)
    Tm = summed("f32", [times(down[1], cc[17]), times(sl(Iw, 15, 143), ke[4]), times(Wb[6], cc[19]), times(Wb[7], ke[7])])
    if anyl:
        KF = tile("f32", 16); ts(KF, KN, F, ALU.mult); kF = [sl(KF, j, j + 1) for j in range(16)]
    Ik = [times(Ib, kn[t]) if any(late[t]) else None for t in range(NV)]
    nIk = [timev(Ib, kn[t], -1.0) if t and any(late[t]) else None for t in range(NV)]
    Wr = [times(Wb[t], 1.0 / S) if not all(late[t]) else None for t in range(NV)]
    pre = [tile("f32", 128) for _ in segs]; ge = [tile("bf", 144) for _ in segs]
    for h in range(len(segs)):
        mset(pre[h], 0.0); mset(sl(ge[h], 0, 16), 1.0)
    Zw = [[tile("bf", 3 * S) for _ in esegs] for _ in range(NV)]
    for t in range(NV):
        for e, (a, b) in enumerate(esegs):
            if b - a < S: mset(sl(Zw[t][e], b - a, S), 0.0); mset(sl(Zw[t][e], S + b - a, 2 * S), 0.0)

    def zland(t, a, b):
        e = [e for e, (x, y) in enumerate(esegs) if x <= a and b <= y][0]
        return sl(Zw[t][e], 2 * S + a - esegs[e][0], 2 * S + b - esegs[e][0])

    Ls = [tile("u16", Q) for _ in range(NV)]
    Lo_ = [tile("u16", Q) for _ in range(NV)]
    vl = [tile("u16", 16) for _ in range(NV)]
    terms = {}
    Lm0 = tile("hf", Q)
    for h, (q0, q1) in enumerate(esegs):
        zo = (sl(z[0], q0, q1), zland(0, q0, q1))
        if late[0][h]:
            ts(sl(Lm0, q0, q1), sl(L0, q0, q1), -F, ALU.add); terms[h] = [(1, sl(Lm0, q0, q1))]; send([zo], 300)
        else:
            ts(sl(Lo_[0], q0, q1), sl(L0, q0, q1), kn[0], ALU.mult)
            send([zo, (sl(Lo_[0], q0, q1), sl(Ls[0], q0, q1))], 500)
    cp(sl(vl[0], 0, 14), sl(v0, 0, 14))

    tag[0] = "t"
    M = tile("f32", TW); HL = tile("bf", 2 * TW); Ef = tile("hf", V); Xa = tile("bf", V)
    H, Lw = sl(HL, 0, V), sl(HL, TW, TW + V); Mw = sl(M, 0, V + 16)
    mset(sl(M, V, TW), 0.0)
    for j in range(4): cp(sl(Ef, 512 * j, 512 * j + 512), sl(E, 512 * j, 512 * j + 512))
    ab = [tile("u16", 128) for _ in range(2)]; cr = V // cfg["nr"]
    for i in range(cfg["nr"]):
        for j, Wj in enumerate((W0, W1)):
            p = sl(ps(), 0, cr // 16); mm(relist(p, Wj, sl(Ef, cr * i, cr * i + cr))); cp(sl(ab[j], cr // 16 * i, cr // 16 * (i + 1)), p)
    for j in range(4):
        c0, o0 = 512 * j, 32 * j
        move(sl(Xa, c0, c0 + 512), ind(X, sl(ab[0], o0, o0 + 32)))
        tt(sl(H, c0, c0 + 512), ind(X, sl(ab[1], o0, o0 + 32)), sl(Xa, c0, c0 + 512), ALU.max)
        tt(sl(Lw, c0, c0 + 512), ind(X, sl(ab[1], o0, o0 + 32)), sl(Xa, c0, c0 + 512), ALU.min)
    tag[0] = "n"
    for j in range(4):
        p = ps(); mm(grp(p, [(Mi, sl(Ef, 512 * j, 512 * j + 512))])); move(sl(M, 512 * j, 512 * j + 512), p)
    NB = 16 * Q
    fz = tile("bf", Q); fzl = tile("bf", Q); fin = [tile("f32", 2 * (b - a)) for a, b in esegs]; finl = [tile("f32", 2 * (b - a)) for a, b in esegs]

    for t in range(NV):
        last = t == NV - 1
        vcl = tile("hf", Q); xvl = tile("bf", Q); vnl = tile("u16", 16)
        xg, xd, zr = tile("bf", NB), tile("bf", NB), tile("bf", NB); sg = [tile("bf", NB) for _ in range(2)]
        for h, (q0, q1) in enumerate(segs):
            n = q1 - q0; b0, b1 = q0 // 16, q1 // 16; nb = b1 - b0; tag[0] = "w%d%d" % (t, h)
            zh = sl(z[t], q0, q1); vh = sl(vl[t], b0, b1)
            c = tile("u16", n); cp(c, ind(E, vh))
            for a in range(q0, q1, CQ):
                move(sl(xg, 16 * a, 16 * a + 16 * CQ), ind(X, sl(c, a - q0, a - q0 + CQ)), cfg["wmode"][t][a // CQ])
            ch = tile("hf", n); cp(ch, c)
            key = sl(ps(), 0, 128, 1, n)
            for j in range(4):
                ks = range(4 * j, 4 * j + 4); p = ps(); o = 16 * q0 + 4 * n * j
                mm([m for k in ks for m in grp(sl(p, n * (k % 4), n * (k % 4) + n), [(Ib, sl(xg, 16 * q0 + k, 16 * q1, 16)), (nIb, zh)])])
                act(sl(xd, o, o + 4 * n), sl(p, 0, 4 * n), ACT.Abs)
                mm(([(key, sl(Kc, 0, n), Ib, True, False)] if j == 0 else []) +
                   [(sl(key, k, 128, 16), sl(xd, o + n * (k % 4), o + n * (k % 4) + n), G32, False, t == 0 and k == 15) for k in ks])
            tag[0] = "x%d%d" % (t, h)
            if t > 0:
                fl = tile("bf", n); lin(fl, ind(Mw, vh), m16, 0.0)
                mm([(key, fl, J, False, True)])
            scan(sl(pre[h], 0, 128, 1, n), sl(rbig, 0, 128, 1, n), key, ALU.add, ALU.min)
            least = tile("f32", 8); cp(least, sl(pre[h], 15, 128, 16))
            tt(sl(ge[h], 16, 144), ind(least, olast), pre[h], ALU.is_equal)
            oh = sl(ps(), 0, n)
            mm(grp(oh, [(nK0, sl(cq, 0, n)), (sl(ge[h], 15, 143, 1, n), sl(nIb, 0, n, 1, n)), (sl(ge[h], 16, 144, 1, n), sl(Ib, 0, n, 1, n))]))
            vc = tile("hf", n); tt(vc, oh, ch, ALU.mult)
            if late[t][h]:
                p = sl(ps(), 0, n); mm(grp(p, [((Ik[t] if s > 0 else nIk[t]), x) for s, x in terms[h]] + [(Wb[t], vc)]))
                ts(sl(Lo_[t], q0, q1), p, kF[t], ALU.add)
                send([(sl(Lo_[t], q0, q1), sl(Ls[t], q0, q1))], 300)
            p = sl(ps(), 0, nb); mm(tolist(p, vc, Wb, G8, cfg["rl"][0], True))
            vn = tile("u16", nb); cp(vn, p)
            send([(vn, sl(vnl, b0, b1))], 0)
            xv = tile("bf", n); move(xv, ind(X, vn))
            send([(xv, sl(xvl, q0, q1))] + ([] if late[t][h] else [(vc, sl(vcl, q0, q1))]), 300 if late[t][h] else 500)
        fa = tile("bf", Q)
        for e, (a, b) in enumerate(esegs):
            tag[0] = "z%d%d" % (t, e); spread(sl(zr, 16 * a, 16 * b), zland(t, a, b), cfg["zg"][t][e])
        for h, (q0, q1) in enumerate(segs):
            n = q1 - q0; b0, b1 = q0 // 16, q1 // 16; tag[0] = "s%d%d" % (t, h); lt = late[t][h]; sT = cfg["sT"]
            zh = zland(t, q0, q1); vnh = sl(vnl, b0, b1); fix = []
            kk = [k for k in range(16) if lt or k != t]
            G = sl(ps(), 0, 128, 1, n) if sT else sl(ps(), 0, n)
            for i, (win, md) in enumerate(((H, cfg["hmode"][t]), (Lw, cfg["lmode"][t]))):
                for a in range(q0, q1, CQ):
                    o, off, zz = sl(sg[i], 16 * a, 16 * a + 16 * CQ), sl(Ls[t], a, a + CQ), sl(zr, 16 * a, 16 * a + 16 * CQ)
                    if md[a // CQ] == "v": tt(o, ind(win, off), zz, ALU.max)
                    else:
                        raw = tile("bf", 16 * CQ); act(raw, ind(win, off))
                        p = sl(ps(), 0, 16 * CQ); mm(grp(p, [(nIb, zz), (Ib, raw)])); relu(o, p)
                        if cfg["hmode"][t][a // CQ] != cfg["lmode"][t][a // CQ]:
                            go, za = sl(G, a - q0, a - q0 + CQ), sl(zh, a - q0, a - q0 + CQ)
                            fix += [(go, (Bb, nBb)[i], za, False, False)] + ([] if lt else [(go, (nWb, Wb)[i][t], za, False, False)])
                for j in range(4):
                    end = lt and i == 1 and j == 3; ks = kk[4 * j:4 * j + 4]
                    if sT: mm([(G, sl(cq, 0, n), Ib, True, False)] * (i + j == 0) +
                              [(sl(G, k, 128, 16), sl(sg[i], 16 * q0 + k, 16 * q1, 16), (G8, nG8)[i], False, end and k == ks[-1]) for k in ks])
                    else: mm(grp(G, [((Wb, nWb)[i][k], sl(sg[i], 16 * q0 + k, 16 * q1, 16)) for k in ks], i + j == 0, end))
                    if fix and i == 1 and j == 0: mm(fix)
            tag[0] = "f%d%d" % (t, h)
            if not lt:
                eh, el = tile("bf", n), tile("bf", n)
                tt(eh, ind(H, vnh), zh, ALU.max); tt(el, ind(Lw, vnh), zh, ALU.max)
                if sT: mm([(sl(G, t, 128, 16), eh, G8, False, False), (sl(G, t, 128, 16), el, nG8, False, True)])
                else: mm(grp(G, [(Wb[t], eh), (nWb[t], el)], False, True))
            if sT:
                fT = sl(tile("bf", 128), 0, 128, 1, n); act(fT, G, ACT.Sign, -float(TAU[t]))
                p = sl(ps(), 0, n); mm(grp(p, [(fT, sl(Ib, 0, n, 1, n))])); move(sl(fa, q0, q1), p)
            else: act(sl(fa, q0, q1), G, ACT.Sign, -0.5 - TAU[t])
        mu = tile("hf", Q); ul16 = tile("hf", 16); mn = tile("f32", Q); vcs = []; uB = []
        for e, (q0, q1) in enumerate(esegs):
            n = q1 - q0; b0, b1 = q0 // 16, q1 // 16; nb = b1 - b0; tag[0] = "e%d%d" % (t, e); sub = inside(q0, q1, segs)
            zh = zland(t, q0, q1); xv = sl(xvl, q0, q1); lt = late[t][sub[0][0]]

            def fresh(p, W):
                return [] if lt else [(p, W, sl(vcl, q0, q1), False, False)]
            ad, hv = sl(Zw[t][e], 0, n), sl(Zw[t][e], S, S + n)
            p = sl(ps(), 0, n); mm(grp(p, [(nIb, zh), (Ib, xv)])); act(ad, p, ACT.Abs)
            p = sl(ps(), 0, n); mm(grp(p, [(Ihalf, sl(cq, 0, n)), (Ihalf, zh), (Ihalf, xv)]))
            if cfg["hva"]:
                r1 = tile("f32", n); act(r1, p, None, MAGIC); act(hv, r1, None, -MAGIC)
            else: ts(hv, p, MAGIC, ALU.add, MAGIC, ALU.subtract)
            Lm = tile("hf", n); ts(Lm, sl(Ls[t], q0, q1), -F, ALU.add)
            vn16 = tile("hf", nb); cp(vn16, sl(vnl, b0, b1))
            ul, w, qq = [sl(tile(a, 128), 0, 128, 1, nb) for a in ("hf", "hf", "bf")]; Inb = sl(Ib, 0, nb, 1, nb)
            p = sl(ps(), 0, 128, 1, nb); mm(blocks(p, ad, G8)); ts(ul, p, TH + 0.5, ALU.is_gt, float(S), ALU.mult)
            p = sl(ps(), 0, 128, 1, nb); mm(blocks(p, hv, Wt8)); lin(qq, p, 4.0 * S, 159.5 + 0.5 / V)
            p = sl(ps(), 0, 128, 1, nb)
            mm([(p, sl(Icq[lt], 0, nb, 1, nb), sl(cq, 0, 128, 1, nb), True, False)] + blocks(p, hv, Wt8, False) +
               (blocks(p, Lm, nR8[t], False) if lt else blocks(p, sl(vcl, q0, q1), nG8s, False)))
            mm([(p, sl(nIq, 0, nb, 1, nb), qq, False, True)])
            tt(w, p, ul, ALU.mult)
            p = ps(); pa, pb = sl(p, 0, n), sl(p, 256, 256 + n)
            mm(grp(pa, [(Bb, ad), (T8, sl(fa, q0, q1))]) + grp(pb, [(IrS, Lm)] + [x[1:3] for x in fresh(pb, Wr[t])]))
            ov = tile("hf", 2 * n); oh, vc = sl(ov, 0, n), sl(ov, n, 2 * n); vcs.append(vc)
            ts(oh, pa, thr, ALU.is_gt, float(S), ALU.mult); tt(vc, pb, oh, ALU.mult)
            p = sl(ps(), 0, 2 * nb); pi_, pu = sl(p, 0, nb), sl(p, nb, 2 * nb)
            lst = tolist(p, ov, Wb, G8, cfg["rl"][1]); uB.append(lst[0][1])
            mm(lst + [(pi_, Ib, sl(Qlist, 0, nb), False, False), (pu, Ir8k, vn16, False, False), (pi_, ul, Inb, False, False), (pu, w, Inb, False, True)])
            iu = tile("u16", 2 * nb); ts(iu, p, F, ALU.add); idx, ue = sl(iu, 0, nb), sl(iu, nb, 2 * nb)
            if cfg["t1a"] and not last:
                t1 = tile("f32", nb); act(t1, pu, ACT.Relu, 0.0, 8192.0)
            else:
                t1 = tile("hf", nb); ts(t1, pu, 8192.0, ALU.mult, 0.0, ALU.max)
            m32 = tile("f32", n); move(m32, ind(Mw, ue))
            muh = sl(mu, q0, q1); ts(muh, m32 if cfg["mum"] else ind(Mw, ue), m012, ALU.mult, -F, ALU.add)
            zn = sl(fz if last else z[t + 1], q0, q1); move(zn, ind(sl(Zw[t][e], 0, 2 * S + n), idx))
            if last:
                send([(zn, sl(fzl, q0, q1))], 300)
                dma("G", dram("yz", (A_, slice(q0, q1))), sl(fzl, q0, q1), 2600)
                p = sl(ps(), 0, n)
                mm([(p, Ihalf, sl(cq, 0, n), True, False)] + [(sl(p, m, n, 16), down[m], t1, False, False) for m in range(16)]); mm([(p, Ib, muh, False, True)])
                lin(sl(fin[e], n, 2 * n), p, 1.0, F + 0.25)
            else:
                if not cfg["zl"]: send([(zn, zland(t + 1, q0, q1))], 300)
                p = sl(ps(), 0, nb); mm(tolist(p, muh, W0, G80, cfg["rl"][2]) + [(p, I32 if cfg["t1a"] else Ib, t1, False, True)]); ts(sl(vl[t + 1], b0, b1), p, F, ALU.add)
            p = sl(ps(), 0, n); mm(grp(p, [(R0r, muh)])); oa = tile("hf", n); tt(oa, p, oh, ALU.mult)
            for h, a, b in sub: terms[h] = [(s, sl(x, a - q0, b - q0)) for s, x in ((1, Lm), (-1, vc), (1, oa))]
            now = [(h, a, b) for h, a, b in sub if last or not late[t + 1][h] or not late[t][h]]
            if now:
                p = sl(ps(), 0, n); mm([(p, Ib, Lm, True, False)] + fresh(p, Wb[t]) + grp(p, [(nIb, vc), (Ib, oa)], False, True))
            if last:
                lin(sl(fin[e], 0, n), p, 1.0, F)
                send([(fin[e], finl[e])], 800)
                dma("S", dram("yl", (A_, slice(q0, q1))), sl(finl[e], 0, n), 2200)
                dma("A", dram("yv", (A_, slice(q0, q1))), ("rows", sl(finl[e], n, 2 * n), 0, n), 2200, [sl(finl[e], n, 2 * n)])
            else:
                if len(now) == len(sub) and not any(late[t + 1][h] for h, a, b in now): now = [(now[0][0], q0, q1)]
                for h, a, b in now:
                    if late[t + 1][h]:
                        Lx = tile("hf", b - a); cp(Lx, sl(p, a - q0, b - q0)); terms[h] = [(1, Lx)]
                    else:
                        ts(sl(Lo_[t + 1], a, b), sl(p, a - q0, b - q0), F, ALU.add, kn[t + 1], ALU.mult)
                        send([(sl(Lo_[t + 1], a, b), sl(Ls[t + 1], a, b))] + [(zn, zland(t + 1, q0, q1))] * cfg["zl"], 300 + 200 * cfg["zl"])
            tag[0] = "g%d%d" % (t, e)
            if not byB: ts(sl(ul16, b0, b1), ue, -F, ALU.add)
            p = sl(ps(), 0, n); mm(grp(p, [(Tm, m32)])); lin(sl(mn, q0, q1), p, 1.0, ke[4])
        news = []
        for u, (q0, q1) in enumerate(esegs if last and cfg["ulast"] else usegs):
            n = q1 - q0; b0, b1 = q0 // 16, q1 // 16; nb = b1 - b0; tag[0] = "u%d%d" % (t, u)
            p = sl(ps(), 0, n); uh = sl(ul16, b0, b1)
            mm([(p, Ib, sl(TriD, 0, n), True, False)] +
               [m for e, a, b in inside(q0, q1, esegs) for m in ((sl(p, a - q0, b - q0), nBr, vcs[e], False, False),
                                                                 (sl(p, a - q0 + 15, b - q0, 16), Br, sl(vcs[e], 15, b - a, 16), False, False))])
            parts = inside(q0, q1, esegs)
            if byB: mm([(sl(p, a - q0, b - q0), uB[e], Rb[b - a], False, b == q1) for e, a, b in parts])
            else: mm([(sl(p, m, n, 16), IrS, uh, False, m == 14) for m in range(15)])
            prod = tile("bf", n); scan(prod, sl(rone, 0, n), p, ALU.add, ALU.mult)
            tq = tile("hf", nb); ts(tq, sl(prod, 14, n, 16), 0.0, ALU.is_equal, 4096.0, ALU.mult)
            p = sl(ps(), 0, nb)
            if byB: mm([(p, Ib, tq, True, False)] + [(sl(p, (a - q0) // 16, (b - q0) // 16), uB[e], sl(Ib, (b - a) // 16, (b - a) // 8, 1, (b - a) // 8), False, b == q1) for e, a, b in parts])
            else: mm(grp(p, [(Ib, uh), (Ib, tq)]))
            so = tile("u16", 2 * nb); ts(sl(so, 0, 2 * nb, 2), p, spare, ALU.min, F, ALU.add)
            news.append((so, q0, nb))
            if not last:
                s16 = tile("hf", nb); ts(s16, p, spare, ALU.min)
                p = sl(ps(), 0, 2 * nb); mm([(sl(p, j, 2 * nb, 2), twice[j], s16, True, True) for j in range(2)])
                so2 = tile("u16", 2 * nb); ts(so2, p, rTW, ALU.add)
                p = sl(ps(), 0, 2 * nb); mm(grp(p, [(pair[s], sl(mu, q0 + s, q1, 8)) for s in range(8)]))
                nl = tile("u16", 2 * nb); ts(nl, p, F, ALU.add)
                xab, rr = tile("bf", 2 * n), tile("bf", 2 * n); move(xab, ind(X, nl))
                p = sl(ps(), 0, n); mm(grp(p, [(nIb, sl(xab, 0, 2 * n, 2)), (Ib, sl(xab, 1, 2 * n, 2))]))
                relu(sl(rr, 0, 2 * n, 2), p); lin(sl(rr, 1, 2 * n, 2), sl(rr, 0, 2 * n, 2), -1.0, 0.0, "V")
                news[-1] += (so2, xab, rr)
        for h, nw in enumerate(news):
            so, q0, nb = nw[:3]; tag[0] = "m%d%d" % (t, h)
            for b in range(nb): cp(ind(M, sl(so, 2 * b, 2 * b + 1)), sl(mn, q0 + 16 * b, q0 + 16 * b + 16))
            if not last:
                so2, xab, rr = nw[3:]; tag[0] = "h%d%d" % (t, h)
                for b in range(nb): tt(ind(HL, sl(so2, 2 * b, 2 * b + 2)), sl(xab, 32 * b, 32 * b + 32), sl(rr, 32 * b, 32 * b + 32), ALU.add)
    dma("S", dram("ya", (A_, A_)), ("rows", M, 6, V), 2400, [sl(M, 0, V)])

    n = len(ops); tls = [o["tiles"] for o in ops]; peek = cfg["peek"]; cases = cfg["cases"]; hop = cases[0][7]
    reach = []; dep = []
    for i in range(n):
        hard = [j for j, h in ops[i]["deps"].items() if h]; below = 0
        for j in hard: below |= reach[j]
        dep.append([(j, h) for j, h in ops[i]["deps"].items() if not below >> j & 1])
        for j in hard: below |= 1 << j
        reach.append(below)
    eng, cost, lat = [None] * n, [0.0] * n, [0.0] * n
    costs = [[0.0] * n for _ in cases]; lats = [[o["lat"][0] * c[5] + o["lat"][1] * c[6] for o in ops] for c in cases]
    pred, succ, back, bsucc = [], [], [], []

    def choose(pick):
        for i, o in enumerate(ops):
            a = o["alts"][pick[i]]; eng[i] = a[0]
            for c, cs in zip(cases, costs): cs[i] = sum(x * y for x, y in zip(a[3], c))
        cost[:] = costs[0]; lat[:] = lats[0]; same = cases[0][8]
        pred[:] = [[(j, cost[j] + lat[j] + (same if eng[j] == eng[i] else hop) if h else 0.0) for j, h in dep[i]] for i in range(n)]
        succ[:] = [[] for _ in range(n)]; bsucc[:] = [[] for _ in range(n)]
        for i in range(n):
            for j, w in pred[i]: succ[j].append((i, w))
        back[:] = [[(i, max(0.0, w - cost[j]) + cost[i] if w else 0.0) for i, w in succ[j]] for j in range(n)]
        for j in range(n):
            for i, w in back[j]: bsucc[i].append((j, w))

    def judge(f):
        if not f: return None
        more = {}; out = []
        for i, j in f[4]: more.setdefault(i, []).append((j, eng[j] != eng[i]))
        for c, cs, ls in zip(cases, costs, lats):
            st = [0.0] * n; free = {e: 0.0 for e in "VAPGS"}; end = 0.0; hp, sm = c[7], c[8]
            for i in f[2]:
                e = eng[i]; s = free[e]
                for j, h in dep[i] + more[i] if i in more else dep[i]:
                    if h:
                        x = st[j] + cs[j] + ls[j] + (sm if eng[j] == e else hp)
                        if x > s: s = x
                st[i] = s; free[e] = s + cs[i]
                if s + cs[i] + ls[i] > end: end = s + cs[i] + ls[i]
            out.append(end)
        return (sum(x / c[9] for x, c in zip(out, cases)) / len(cases) * cases[0][9] + fullest(),) + f[1:] + (out,)

    def fullest():
        return cfg["even"] * max(sum(c for c, e in zip(costs[0], eng) if e == x) for x in "VA")
    uses = {tl: len(set(a[0] for a in lst)) for tl, lst in psacc.items()}

    def run(pr, pre_, suc_, av0, banks=8):
        left = dict(uses); bank, held, lastuse, bfree, extra = {}, [None] * banks, [[] for _ in range(banks)], [0.0] * banks, []
        miss = [len(x) for x in pre_]; st = [0.0] * n; av = list(av0); free = {e: 0.0 for e in "VAPGS"}; order = []
        ready = {e: [i for i in range(n) if miss[i] == 0 and eng[i] == e] for e in "VAPGS"}
        for step in range(n):
            fb = [x for x in range(banks) if held[x] is None]; b0 = min(fb, key=lambda x: bfree[x]) if fb else None
            s0 = 1e18; e0 = None; bf = bfree[b0] if fb else 1e18
            for e, lst in ready.items():
                for i in lst:
                    s = av[i]
                    if tls[i] and tls[i][0] not in bank and bf > s: s = bf
                    if free[e] > s: s = free[e]
                    if s < s0: s0, e0 = s, e
            if s0 >= 1e18: return None
            i = -1; lim = s0 + peek
            for k in ready[e0]:
                if av[k] <= lim and (i < 0 or pr[k] > pr[i]) and not (tls[k] and tls[k][0] not in bank and bf > lim): i = k
            s = max(av[i], free[e0])
            if tls[i]:
                tl = tls[i][0]
                if tl not in bank:
                    s = max(s, bf); bank[tl] = b0; held[b0] = tl
                    extra += [(i, j) for j in lastuse[b0]]; lastuse[b0] = []
                b = bank[tl]; lastuse[b].append(i); left[tl] -= 1; bfree[b] = max(bfree[b], s + cost[i] + lat[i] + hop)
                if left[tl] == 0: held[b] = None
            st[i] = s; free[e0] = s + cost[i]; order.append(i); ready[e0].remove(i)
            for j, w in suc_[i]:
                if s + w > av[j]: av[j] = s + w
                miss[j] -= 1
                if miss[j] == 0: ready[eng[j]].append(j)
        return max(st[i] + cost[i] + lat[i] for i in range(n)), st, order, bank, extra
    zero = [0.0] * n; rnd = [cfg["seed"]]
    kind_ = [o["tag"] + o["eng"] for o in ops]; tags = sorted(set(kind_))
    free_ = [i for i, o in enumerate(ops) if len(o["alts"]) > 1]; pick = [0] * n; choose(pick)

    def draw():
        rnd[0] = (rnd[0] * 6364136223846793005 + 1442695040888963407) % 2 ** 64
        return (rnd[0] >> 33) / 2.0 ** 31
    pr = [0.0] * n; after = {}
    for i in range(n - 1, -1, -1):
        pr[i] = max([pr[j] + w for j, w in succ[i]] + [cost[i] + lat[i]] + ([pr[after[kind_[i]]] + cost[i]] if kind_[i] in after else []))
        after[kind_[i]] = i
    best = cur = judge(run(pr, pred, succ, zero)); curp = pr; bestpick = pick; now = pick
    for it in range(cfg["rounds"]):
        p3 = pick
        if draw() < cfg["pflip"]:
            p3 = list(pick)
            for _ in range(1 + int(2 * draw())):
                i = free_[int(len(free_) * draw())]; p3[i] = (p3[i] + 1) % len(ops[i]["alts"])
        if p3 is not now: choose(p3); now = p3
        if p3 is not pick and cur and draw() < 0.6: p2 = [-x for x in cur[1]]
        elif cur and draw() < cfg["pback"]:
            amp = 2000.0 * draw() ** 2; nz = {tg: amp * (draw() - 0.5) for tg in tags}
            r = run([cur[1][i] + cost[i] + nz[kind_[i]] for i in range(n)], back, bsucc, lat, cfg["bb"])
            p2 = [r[1][i] + cost[i] for i in range(n)] if r else None
        else:
            base = [-x for x in cur[1]] if cur and draw() < 0.5 else curp
            nz = {tg: 0.0 for tg in tags}
            for _ in range(1 + int(3 * draw())): nz[tags[int(len(tags) * draw())]] = 6000.0 * draw() ** 2 * (1 if draw() < 0.5 else -1)
            p2 = [base[i] + nz[kind_[i]] for i in range(n)]
        f = judge(run(p2, pred, succ, zero)) if p2 else None
        if f and (best is None or f[0] < best[0]): best, bestpick = f, p3
        if f and (cur is None or f[0] < cur[0] + cfg["temp"] * (1.0 - it / cfg["rounds"]) * draw()): cur, curp, pick = f, p2, p3
    _, st_t, order, bank, extra, ends = best; choose(bestpick)
    alld = [list(d) for d in dep]
    for i, j in extra: alld[i].append((j, 2))
    outs = [[] for _ in range(n)]
    for i in range(n):
        for j, h in alld[i]: outs[j].append(i)

    def replay(seq):
        miss = [len(d) for d in alld]; at = {e: 0 for e in seq}; od = []; go_ = True
        while go_:
            go_ = False
            for e, q in seq.items():
                k = at[e]
                while k < len(q) and miss[q[k]] == 0:
                    od.append(q[k])
                    for j in outs[q[k]]: miss[j] -= 1
                    k += 1
                if k > at[e]: at[e] = k; go_ = True
        if len(od) < n: return None
        res = []
        for c, cs, ls in zip(cases, costs, lats):
            st = [0.0] * n; why = [-1] * n; free = {e: (0.0, -1) for e in seq}; end = 0.0; hp, sm = c[7], c[8]; top_ = 0
            for i in od:
                e = eng[i]; s, y = free[e]
                for j, h in alld[i]:
                    if h == 1 or (h and eng[j] != e):
                        x = st[j] + cs[j] + ls[j] + (sm if eng[j] == e else hp)
                        if x > s: s, y = x, j
                st[i] = s; why[i] = y; s += cs[i]; free[e] = (s, i)
                if s + ls[i] > end: end, top_ = s + ls[i], i
            res.append((end, st, why, top_))
        return sum(r[0] / c[9] for r, c in zip(res, cases)) / len(cases) * cases[0][9] + fullest(), od, res

    def seteng(i, k):
        a = ops[i]["alts"][k]; eng[i] = a[0]
        for c, cs in zip(cases, costs): cs[i] = sum(x * y for x, y in zip(a[3], c))
    seq = {e: [i for i in order if eng[i] == e] for e in "VAPGS"}; pick = list(bestpick)
    cur = replay(seq); best = (cur, dict(seq), list(pick))
    for it in range(cfg["polish"]):
        end, st, why, i = cur[2][int(len(cases) * draw())]; path = []
        while i >= 0: path.append(i); i = why[i]
        i = path[int(len(path) * draw())]; e = eng[i]; q = seq[e]; k = q.index(i); new = dict(seq); u = draw(); old = pick[i]
        if len(ops[i]["alts"]) > 1 and u < 0.3:
            pick[i] = (old + 1) % len(ops[i]["alts"]); seteng(i, pick[i]); new[e] = q[:k] + q[k + 1:]; q2 = seq[eng[i]]
            k2 = max(0, sum(1 for j in q2 if st[j] < st[i]) - int(2 * draw())); new[eng[i]] = q2[:k2] + [i] + q2[k2:]
        elif u < 0.7:
            d = 1 + int(4 * draw() ** 2); k2 = max(0, k - d); new[e] = q[:k2] + [i] + q[k2:k] + q[k + 1:]
        else:
            d = 1 + int(4 * draw() ** 2); new[e] = q[:k] + q[k + 1:k + 1 + d] + [i] + q[k + 1 + d:]
        f = replay(new)
        if f and f[0] < cur[0] + cfg["temp2"] * (1.0 - it / cfg["polish"]) * draw():
            cur, seq = f, new
            if f[0] < best[0][0]: best = (f, dict(new), list(pick))
        elif pick[i] != old: pick[i] = old; seteng(i, old)
    bestpick = best[2]; choose(bestpick); order = best[0][1]; st_t = best[0][2][0][1]; ends = [r[0] for r in best[0][2]]; best = best[0]
    order = sorted(order, key=lambda i, pos={j: k for k, j in enumerate(order)}: (st_t[i], pos[i]))
    for i, o in enumerate(ops): o["eng"], o["kind"], o["args"] = o["alts"][bestpick[i]][:3]; o["cost"] = cost[i]
    fin_t = [st_t[i] + cost[i] + lat[i] for i in range(n)]
    for i, j in extra: ops[i]["deps"][j] = ops[i]["deps"].get(j, False) or eng[j] != eng[i]

    need = set(j for o in ops for j, hard in o["deps"].items() if hard)
    cnt = {e: 0 for e in "VAPG"}; sig = {}; nd = [0]
    for i in order:
        o = ops[i]
        if o["dma"]: sig[i] = ("d%d" % nd[0], 1); nd[0] += 1
        elif i in need: cnt[o["eng"]] += 1; sig[i] = ("c" + o["eng"], cnt[o["eng"]])
    know = {e: {} for e in "VAPGS"}; clock = {}; prog = []
    for i in order:
        o = ops[i]; kn_ = know[o["eng"]]; waits = []
        for j in sorted([j for j, hard in o["deps"].items() if hard], key=lambda j: -fin_t[j]):
            sname, val = sig[j]
            if kn_.get(sname, 0) >= val: continue
            waits.append(j)
            for a, b in clock[j].items(): kn_[a] = max(kn_.get(a, 0), b)
        if i in sig:
            clock[i] = {} if o["kind"] == "send" else dict(kn_)
            clock[i][sig[i][0]] = sig[i][1]
        prog.append((o, [(sig[j], ops[j]) for j in waits], sig.get(i)))
    return {"prog": prog, "bank": bank, "top": top, "cnt": cnt, "nd": nd[0], "end": max(fin_t), "ops": ops, "st": st_t, "fin": fin_t, "order": order, "ends": ends, "score": best[0]}


PLAN = plan(CFG)
SCRATCH = {"s_" + a: ("sbuf", [128, (PLAN["top"][a] + 15) // 16 * 16], DT[a]) for a in DT}
SCRATCH.update({"ps%d" % b: ("psum", [128, 512], "float32") for b in range(8)})
SEMAPHORES = ["cV", "cA", "cP", "cG", "sent"] + ["d%d" % i for i in range(PLAN["nd"])]


def masks(topo, src, dst, n):
    e = topo.engines(src, dst); k = len(e) // n
    return [sum(1 << x for x in e[k * j:k * j + k]) for j in range(n)], k


def rank_program(g, core, T, topo):
    rank = T.rank_of(core)
    if rank is None:
        return
    N = len(T.cores); nxt = T.cores[(rank + 1) % N]; prv = T.cores[(rank - 1) % N]
    rid, pid = topo.addr(nxt, core)
    Qs = {"V": g.vector, "A": g.scalar, "P": g.tensor, "G": g, "S": g.sync}

    def ap(r):
        if not isinstance(r, tuple): return r
        if r[0] == "ind": return ap(r[1]).indirect(ap(r[2]))
        if r[0] == "dram": return T[r[1]][r[2]]
        if r[0] == "rows": return T["s_" + r[1][0]][r[2]:128:16, r[1][1]:r[1][1] + r[3]]
        buf = T["ps%d" % PLAN["bank"][r[5]]] if r[0] == "ps" else T["s_" + r[0]]
        return buf[0:r[4], r[1]:r[2]] if r[3] == 1 else buf[0:r[4], r[1]:r[2]:r[3]]

    def total(o):
        if o["kind"] == "dma": return 16
        return masks(topo, prv, core, len(o["args"]))[1] * len(o["args"])

    sent = [0]; tail = []
    for o, waits, sig in PLAN["prog"]:
        q = Qs[o["eng"]]; a = o["args"]; k = o["kind"]
        for (name, val), src in waits:
            q.wait_ge(T.sem[name], total(src) if src["dma"] else val)
        if k == "send":
            ms, ne = masks(topo, core, nxt, len(a)); sent[0] += ne * len(a)
            if len(a) == 1:
                g.remote_dma(ap(a[0][1]), ap(a[0][0]), T.sem[sig[0]], T.sem.sent, pid, rid, ms[0])
            else:
                g.remote_dma_fused([RemoteDMATransfer(dst_ids=[DstId(rid=rid, pnc=pid)], dma_engine_mask=m, remote_sem=T.sem[sig[0]],
                                                      src=ap(s), dst=ap(d)) for m, (s, d) in zip(ms, a)], local_sem=T.sem.sent)
            tail.append((sig[0], total(o)))
            continue
        if k == "dma":
            q.dma_start(ap(a[0]), ap(a[1])).then_inc(T.sem[sig[0]], 16); tail.append((sig[0], 16))
            continue
        if k == "cp": ins = q.tensor_copy(ap(a[0]), ap(a[1]))
        elif k == "tt": ins = q.tensor_tensor(ap(a[0]), ap(a[1]), ap(a[2]), a[3])
        elif k == "ts":
            ins = q.tensor_scalar(ap(a[0]), ap(a[1]), ap(a[2]), None, a[4]) if a[5] is None else \
                q.tensor_scalar(ap(a[0]), ap(a[1]), ap(a[2]), ap(a[3]), a[4], a[5])
        elif k == "scan": ins = q.tensor_tensor_scan(ap(a[0]), ap(a[1]), ap(a[2]), 0.0, a[3], a[4])
        elif k == "mset": ins = q.memset(ap(a[0]), a[1])
        elif k == "act": ins = q.activation(ap(a[0]), ap(a[1]), a[2], bias=ap(a[3]), scale=ap(a[4]))
        elif k == "asel": ins = q.affine_select(ap(a[0]), ap(a[1]), a[2], a[3], a[4], a[5], a[6])
        elif k == "iota":
            ins = q.iota(ap(a[0]), a[1], a[2], a[3]) if a[0][0] == "i32" else q.iota(ap(a[0]), a[1], a[2], a[3], allow_small_or_imprecise_dtypes=True)
        else:
            for m in a: ins = q.matmul(ap(m[0]), ap(m[1]), ap(m[2]), m[3], m[4])
        if sig: ins.then_inc(T.sem[sig[0]], 1)
    for e in "VAPG":
        if PLAN["cnt"][e]: g.wait_ge(T.sem["c" + e], PLAN["cnt"][e])
    g.wait_ge(T.sem.sent, sent[0])
    for name, val in tail: g.wait_ge(T.sem[name], val)
